import numpy as np
import ml_dtypes


def mxq(x, axis, fmt="e4m3"):
    dtype, down = {"e4m3": (ml_dtypes.float8_e4m3fn, 7), "e5m2": (ml_dtypes.float8_e5m2, 14)}[fmt]
    v = np.moveaxis(np.asarray(x, np.float32).astype(ml_dtypes.bfloat16).astype(np.float64), axis, -1)
    blocks = v.reshape(v.shape[:-1] + (-1, 32))
    amax = np.abs(blocks).max(-1, keepdims=True)
    byte = np.maximum(np.where(amax > 0, np.frexp(amax)[1] - 1 + 127, 0) - down, 1)
    scale = np.exp2(byte - 127.0)
    codes = (blocks / scale).astype(np.float32).astype(dtype).astype(np.float64)
    return np.moveaxis((codes * scale).reshape(v.shape), -1, axis)


WIDE = False


def mx_kscale(k):
    if not WIDE:
        return np.ones(k)
    levels = np.array([10, -10, 5, -5, 0])
    if k % 512:
        return np.exp2(np.random.permutation(np.resize(levels, k // 32))).repeat(32)
    a = np.empty((k // 512, 16))
    for p in range(k // 512):
        a[p, :8] = np.random.permutation(np.resize(levels, 8))
        for g in range(8):
            far = levels[np.abs(levels - a[p, g]) >= 10]
            a[p, g + 8] = far[np.random.randint(len(far))]
    return np.exp2(a.ravel()).repeat(32)


def f64(x):
    return np.asarray(x).astype(np.float64)


def striped(idx):
    return np.tile(idx.reshape(-1, 16).T, (8, 1)).astype(np.uint16)


def unstriped(offs):
    return offs[:16].T.reshape(-1).astype(np.int64)


E2M1 = np.array([0.0, 0.5, 1.0, 1.5, 2.0, 3.0, 4.0, 6.0, -0.0, -0.5, -1.0, -1.5, -2.0, -3.0, -4.0, -6.0])


def pack_fp4(w):
    k, n = w.shape
    w = f64(np.asarray(w, np.float32).astype(ml_dtypes.bfloat16)).reshape(k // 32, 32, n)
    amax = np.abs(w).max(1)
    mant, ex = np.frexp(amax / 6.0)
    byte = np.clip(np.where(amax > 0, np.where(mant > 0.5, ex, ex - 1) + 127, 1), 1, 254)
    scaled = (w * np.exp2(127.0 - byte)[:, None, :]).reshape(k, n).astype(np.float32)
    c = np.ascontiguousarray(scaled.reshape(k // 512, 128, 4, n).transpose(0, 1, 3, 2)).astype(ml_dtypes.float4_e2m1fn).view(np.uint8) & 0xF
    words = (c[..., 0::2] | (c[..., 1::2] << 4)).reshape(k // 512, 128, 2 * n)
    return np.ascontiguousarray(words), np.ascontiguousarray(byte.astype(np.uint8).reshape(k // 512, 16, n))


def unpack_fp4(words, scales):
    g, _, n = scales.shape
    words = np.ascontiguousarray(words).reshape(g, 128, n, 2)
    nib = np.empty((g, 128, n, 4), np.uint8)
    nib[..., 0::2] = words & 0xF
    nib[..., 1::2] = words >> 4
    vals = E2M1[nib] * np.repeat(np.exp2(scales.astype(np.float64) - 127.0), 8, axis=1)[..., None]
    return vals.transpose(0, 1, 3, 2).reshape(g * 512, n)


K, T, S, H, N = 1024, 2048, 512, 512, 256


def setup_inputs():
    n = np.random.standard_normal
    s = mx_kscale(K)[:, None]
    u = mx_kscale(H)
    packed_w2 = pack_fp4(n((H, N)) / np.sqrt(H) / u[:, None])
    return {
        "xT": (n((K, T)) * s).astype(np.float32),
        "w1": (n((K, H)) / np.sqrt(K) / s).astype(np.float32),
        "w2_words": packed_w2[0],
        "w2_scales": packed_w2[1],
        "gamma": (np.random.uniform(0.5, 1.5, (H, 1)) * u[:, None]).astype(np.float32),
        "offs": striped(np.random.permutation(T)[:S]),
    }


def reference(xT, w1, w2_words, w2_scales, gamma, offs):
    xq = mxq(f64(xT)[:, unstriped(offs)], 0, "e4m3")
    h = mxq(f64(w1), 0, "e4m3").T @ xq
    hn = (h - h.mean(axis=1, keepdims=True)) / np.sqrt(h.var(axis=1, keepdims=True) + 1e-5)
    z = f64(gamma) * hn
    return unpack_fp4(w2_words, w2_scales).T @ mxq(z, 0, "e4m3")

@@ -1,0 +1,203 @@
+from contextlib import ExitStack
+
+import concourse.mybir as mybir
+
+K, T, S, H, N = 1024, 2048, 512, 512, 256
+FLOPS = 2 * K * H * S + 2 * H * N * S
+EPS = 1e-5
+
+F32 = mybir.dt.float32
+BF16 = mybir.dt.bfloat16
+I32 = mybir.dt.int32
+U32 = mybir.dt.uint32
+U16 = mybir.dt.uint16
+U8 = mybir.dt.uint8
+FP8X4 = mybir.dt.float8_e4m3fn_x4
+FP4X4 = mybir.dt.float4_e2m1fn_x4
+ACT = mybir.ActivationFunctionType
+ALU = mybir.AluOpType
+
+P = 128
+PACK = 4
+PASSES = K // (P * PACK)
+HALF = S // 2
+M_VECTOR = 88
+
+
+def tile_picked_inorm_none_e_kernel(tc, xT, w1, w2_words, w2_scales, gamma, offs, out):
+    nc = tc.nc
+    with ExitStack() as ctx:
+        keep = ctx.enter_context(tc.tile_pool(name="keep", bufs=1))
+        psum = ctx.enter_context(tc.psum_pool(name="psum", bufs=1))
+
+        def sbuf(name, shape, dtype, tag=None):
+            return keep.tile(shape, dtype, name=name, tag=tag or name, align_bytes=64)
+
+        offsets = keep.tile([P, S // 16], U16, name="offsets")
+        gain = sbuf("gain", [P, PACK], F32)
+        x_rows = xT.rearrange("(g p j) t -> g j p t", p=P, j=PACK)
+        w_rows = w1.rearrange("(g p j) c -> g p j c", p=P, j=PACK)
+
+        x_planes = {}
+        for g in range(PASSES):
+            for j in range(PACK):
+                x_planes[g, j] = sbuf("x_plane%d%d" % (g, j), [P, T], F32)
+                nc.sync.dma_start(out=x_planes[g, j][:], in_=x_rows[g, j])
+                if (g, j) == (0, 0):
+                    nc.sync.dma_start(offsets[:], offs)
+                    nc.sync.dma_start(out=gain[:], in_=gamma.rearrange("(p t) o -> p (t o)", t=PACK))
+        w_raw = []
+        for g in range(PASSES):
+            w_raw.append(sbuf("w_raw%d" % g, [P, PACK, H], F32))
+            nc.sync.dma_start(out=w_raw[g][:], in_=w_rows[g])
+        w2_codes = sbuf("w2_codes", [P, 2 * N], U8)
+        nc.sync.dma_start(out=w2_codes[:].bitcast(I32), in_=w2_words[0].bitcast(I32))
+        w2_plane = sbuf("w2_plane", [P, N], U8)
+        nc.gpsimd.memset(w2_plane[:], 0)
+        for q in range(4):
+            nc.sync.dma_start(
+                out=w2_plane[32 * q : 32 * q + 4, :].bitcast(I32),
+                in_=w2_scales[0, 4 * q : 4 * q + 4, :].bitcast(I32),
+            )
+
+        neg_gain = sbuf("neg_gain", [P, PACK], F32)
+        nc.gpsimd.tensor_scalar(neg_gain[:], gain[:], -1.0, 0.0, ALU.mult, ALU.add)
+        moments = []
+        for t in range(PACK):
+            moments.append(sbuf("moments%d" % t, [P, 3], F32))
+            nc.vector.memset(moments[t][:, 0:1], -1.0)
+
+        x_codes, x_scales = [], []
+        for g in range(PASSES):
+            picked = sbuf("picked%d" % g, [P, S, PACK], BF16, tag="staging%d" % g)
+            for j in range(PACK):
+                nc.vector.tensor_copy(picked[:, :, j], x_planes[g, j][:].indirect(offsets[:]))
+            x_codes.append(sbuf("x_codes%d" % g, [P, S], U32))
+            x_scales.append(sbuf("x_scales%d" % g, [P, S], U8))
+            nc.vector.quantize_mx(
+                out=x_codes[g][:].bitcast(FP8X4),
+                scales=x_scales[g][:],
+                in_=picked[:].rearrange("p s j -> p (s j)"),
+            )
+
+        spans = {t: [slice(0, S)] if t == 0 else [slice(0, HALF), slice(HALF, S)] for t in range(PACK)}
+        hidden = {}
+        for t in range(PACK):
+            for piece, cols in enumerate(spans[t]):
+                hidden[t, piece] = psum.tile(
+                    [P, cols.stop - cols.start], F32, name="hidden%d%d" % (t, piece), tag="bank%d%d" % (t, piece)
+                )
+
+        partial = {t: sbuf("partial%d" % t, [P, 2, 6], F32) for t in range(1, PACK)}
+
+        for g in range(PASSES):
+            dealt = sbuf("dealt%d" % g, [P, PACK, P, PACK], BF16, tag="staging%d" % (PASSES - 1))
+            source = w_raw[g][:].rearrange("p j (m t) -> p m j t", t=PACK)
+            target = dealt[:].rearrange("p t m j -> p m j t")
+            nc.vector.tensor_copy(out=target[:, :M_VECTOR], in_=source[:, :M_VECTOR])
+            nc.scalar.copy(out=target[:, M_VECTOR:], in_=source[:, M_VECTOR:])
+            for t in range(PACK):
+                w_codes = sbuf("w_codes%d%d" % (g, t), [P, P], U32)
+                w_scales = sbuf("w_scales%d%d" % (g, t), [P, P], U8)
+                nc.vector.quantize_mx(
+                    out=w_codes[:].bitcast(FP8X4),
+                    scales=w_scales[:],
+                    in_=dealt[:, t].rearrange("p m j -> p (m j)"),
+                )
+                for piece, cols in enumerate(spans[t]):
+                    nc.tensor.matmul_mx(
+                        out=hidden[t, piece][:],
+                        lhsT=w_codes[:].bitcast(FP8X4),
+                        lhsT_scale=w_scales[:],
+                        rhs=x_codes[g][:, cols].bitcast(FP8X4),
+                        rhs_scale=x_scales[g][:, cols],
+                        start=(g == 0),
+                        stop=(g == PASSES - 1),
+                    )
+
+        z_planes = sbuf("z_planes", [P, PACK, S], BF16)
+        affine = {}
+        inv_std = {}
+
+        def coefficients(t, engine):
+            affine[t] = sbuf("affine%d" % t, [P, 2], F32)
+            engine.tensor_scalar(
+                affine[t][:], moments[t][:, 0:2], inv_std[t][:], neg_gain[:, t : t + 1], ALU.mult, ALU.mult
+            )
+
+        first = sbuf("first", [P, S], F32)
+        squares = sbuf("squares", [P, S], F32)
+        sums = sbuf("sums", [P, 2], F32)
+        nc.scalar.activation(first[:], hidden[0, 0][:], ACT.Identity, accum_out=sums[:, 0:1])
+        nc.scalar.activation(moments[0][:, 1:2], sums[:, 0:1], ACT.Copy, scale=1.0 / S)
+        nc.scalar.activation(
+            squares[:], hidden[0, 0][:], ACT.Square, bias=moments[0][:, 1:2], scale=-1.0, accum_out=sums[:, 1:2]
+        )
+        inv_std[0] = sbuf("inv_std0", [P, 1], F32)
+        nc.scalar.activation(inv_std[0][:], sums[:, 1:2], ACT.Abs_reciprocal_sqrt, bias=EPS, scale=1.0 / S)
+        coefficients(0, nc.gpsimd)
+
+        for t in range(1, PACK):
+            for half in range(2):
+                nc.vector.bn_stats(partial[t][:, half, :], hidden[t, half][:])
+            nc.vector.bn_aggr(moments[t][:, 1:3], partial[t][:].rearrange("p h s -> p (h s)"))
+            inv_std[t] = sbuf("inv_std%d" % t, [P, 1], F32)
+            nc.scalar.activation(inv_std[t][:], moments[t][:, 2:3], ACT.Abs_reciprocal_sqrt, bias=EPS)
+            coefficients(t, nc.gpsimd if t == 1 else nc.vector)
+
+        def normalise_vector(t, source, cols):
+            nc.vector.tensor_scalar(
+                z_planes[:, t, cols], source, affine[t][:, 0:1], affine[t][:, 1:2], ALU.mult, ALU.add
+            )
+
+        def normalise_scalar(t, source, cols):
+            nc.scalar.activation(
+                z_planes[:, t, cols], source, ACT.Identity, bias=affine[t][:, 1:2], scale=affine[t][:, 0:1]
+            )
+
+        normalise_vector(0, first[:], slice(0, S))
+        for t in range(1, PACK):
+            for half, cols in enumerate(spans[t]):
+                if (t, half) == (PACK - 1, 1):
+                    normalise_vector(t, hidden[t, half][:], cols)
+                else:
+                    normalise_scalar(t, hidden[t, half][:], cols)
+
+        woven = [sbuf("woven%d" % half, [P, HALF, PACK], BF16) for half in range(2)]
+
+        def weave(copy, half, start, stop):
+            copy(
+                out=woven[half][:, start:stop, :].rearrange("p (c i) t -> p c t i", i=4),
+                in_=z_planes[:, :, half * HALF + start : half * HALF + stop].rearrange("p t (c i) -> p c t i", i=4),
+            )
+
+        weave(nc.vector.tensor_copy, 0, 0, HALF)
+        weave(nc.vector.tensor_copy, 1, 0, HALF // 2)
+        weave(nc.scalar.copy, 1, HALF // 2, HALF)
+        out_rows = out.rearrange("(m p) s -> m p s", p=P)
+        for half in range(2):
+            cols = slice(half * HALF, (half + 1) * HALF)
+            z_codes = sbuf("z_codes%d" % half, [P, HALF], U32)
+            z_scales = sbuf("z_scales%d" % half, [P, HALF], U8)
+            nc.vector.quantize_mx(
+                out=z_codes[:].bitcast(FP8X4),
+                scales=z_scales[:],
+                in_=woven[half][:].rearrange("p s t -> p (s t)"),
+            )
+            for m in range(N // P):
+                acc = psum.tile([P, HALF], F32, name="acc%d%d" % (m, half), tag="bank%d%d" % (m + 1, half))
+                nc.tensor.matmul_mx(
+                    out=acc[:],
+                    lhsT=w2_codes[:, 2 * P * m : 2 * P * (m + 1)].bitcast(FP4X4),
+                    lhsT_scale=w2_plane[:, P * m : P * (m + 1)],
+                    rhs=z_codes[:].bitcast(FP8X4),
+                    rhs_scale=z_scales[:],
+                    start=True,
+                    stop=True,
+                )
+                result = sbuf("result%d%d" % (m, half), [P, HALF], F32)
+                if m == 1:
+                    nc.vector.tensor_copy(out=result[:], in_=acc[:])
+                else:
+                    nc.scalar.copy(out=result[:], in_=acc[:])
+                nc.sync.dma_start(out=out_rows[m][:, cols], in_=result[:])

@@ -22,6 +22,8 @@ PACK = 4
 PASSES = K // (P * PACK)
 HALF = S // 2
 M_VECTOR = 88
+CHUNK = 128
+SCALAR_PLANE = 1
 
 
 def tile_picked_inorm_none_e_kernel(tc, xT, w1, w2_words, w2_scales, gamma, offs, out):
@@ -35,21 +37,28 @@ def tile_picked_inorm_none_e_kernel(tc, xT, w1, w2_words, w2_scales, gamma, offs
 
         offsets = keep.tile([P, S // 16], U16, name="offsets")
         gain = sbuf("gain", [P, PACK], F32)
-        x_rows = xT.rearrange("(g p j) t -> g j p t", p=P, j=PACK)
+        x_rows = xT.rearrange("(g p j) t -> g p j t", p=P, j=PACK)
         w_rows = w1.rearrange("(g p j) c -> g p j c", p=P, j=PACK)
 
         x_planes = {}
         for g in range(PASSES):
-            for j in range(PACK):
-                x_planes[g, j] = sbuf("x_plane%d%d" % (g, j), [P, T], F32)
-                nc.sync.dma_start(out=x_planes[g, j][:], in_=x_rows[g, j])
-                if (g, j) == (0, 0):
+            rows_per_load = 2 if g == 0 else 1
+            for j0 in range(0, PACK, rows_per_load):
+                loaded = sbuf("x_rows%d%d" % (g, j0), [P, rows_per_load, T], F32)
+                nc.sync.dma_start(out=loaded[:], in_=x_rows[g][:, j0 : j0 + rows_per_load])
+                for j in range(rows_per_load):
+                    x_planes[g, j0 + j] = loaded[:, j, :]
+                if (g, j0) == (0, 0):
                     nc.sync.dma_start(offsets[:], offs)
-                    nc.sync.dma_start(out=gain[:], in_=gamma.rearrange("(p t) o -> p (t o)", t=PACK))
-        w_raw = []
+        w_raw = {}
         for g in range(PASSES):
-            w_raw.append(sbuf("w_raw%d" % g, [P, PACK, H], F32))
-            nc.sync.dma_start(out=w_raw[g][:], in_=w_rows[g])
+            rows_per_load = PACK if g == 0 else 2
+            w_raw[g] = []
+            for j0 in range(0, PACK, rows_per_load):
+                loaded = sbuf("w_rows%d%d" % (g, j0), [P, rows_per_load, H], F32)
+                nc.sync.dma_start(out=loaded[:], in_=w_rows[g][:, j0 : j0 + rows_per_load])
+                w_raw[g].append((slice(j0, j0 + rows_per_load), loaded))
+        nc.sync.dma_start(out=gain[:], in_=gamma.rearrange("(p t) o -> p (t o)", t=PACK))
         w2_codes = sbuf("w2_codes", [P, 2 * N], U8)
         nc.sync.dma_start(out=w2_codes[:].bitcast(I32), in_=w2_words[0].bitcast(I32))
         w2_plane = sbuf("w2_plane", [P, N], U8)
@@ -60,6 +69,10 @@ def tile_picked_inorm_none_e_kernel(tc, xT, w1, w2_words, w2_scales, gamma, offs
                 in_=w2_scales[0, 4 * q : 4 * q + 4, :].bitcast(I32),
             )
 
+        warm_in = sbuf("warm_in", [P, 1], F32)
+        warm_out = sbuf("warm_out", [P, 1], F32)
+        nc.vector.memset(warm_in[:], 1.0)
+        nc.scalar.activation(warm_out[:], warm_in[:], ACT.Abs_reciprocal_sqrt, bias=EPS)
         neg_gain = sbuf("neg_gain", [P, PACK], F32)
         nc.gpsimd.tensor_scalar(neg_gain[:], gain[:], -1.0, 0.0, ALU.mult, ALU.add)
         moments = []
@@ -71,7 +84,7 @@ def tile_picked_inorm_none_e_kernel(tc, xT, w1, w2_words, w2_scales, gamma, offs
         for g in range(PASSES):
             picked = sbuf("picked%d" % g, [P, S, PACK], BF16, tag="staging%d" % g)
             for j in range(PACK):
-                nc.vector.tensor_copy(picked[:, :, j], x_planes[g, j][:].indirect(offsets[:]))
+                nc.vector.tensor_copy(picked[:, :, j], x_planes[g, j].indirect(offsets[:]))
             x_codes.append(sbuf("x_codes%d" % g, [P, S], U32))
             x_scales.append(sbuf("x_scales%d" % g, [P, S], U8))
             nc.vector.quantize_mx(
@@ -80,7 +93,7 @@ def tile_picked_inorm_none_e_kernel(tc, xT, w1, w2_words, w2_scales, gamma, offs
                 in_=picked[:].rearrange("p s j -> p (s j)"),
             )
 
-        spans = {t: [slice(0, S)] if t == 0 else [slice(0, HALF), slice(HALF, S)] for t in range(PACK)}
+        spans = {t: [slice(0, S)] if t == SCALAR_PLANE else [slice(0, HALF), slice(HALF, S)] for t in range(PACK)}
         hidden = {}
         for t in range(PACK):
             for piece, cols in enumerate(spans[t]):
@@ -88,32 +101,41 @@ def tile_picked_inorm_none_e_kernel(tc, xT, w1, w2_words, w2_scales, gamma, offs
                     [P, cols.stop - cols.start], F32, name="hidden%d%d" % (t, piece), tag="bank%d%d" % (t, piece)
                 )
 
-        partial = {t: sbuf("partial%d" % t, [P, 2, 6], F32) for t in range(1, PACK)}
+        partial = {t: sbuf("partial%d" % t, [P, 2, 6], F32) for t in range(PACK) if t != SCALAR_PLANE}
+
+        w_codes, w_scales = {}, {}
+
+        def project(g, t, first):
+            for piece, cols in enumerate(spans[t]):
+                nc.tensor.matmul_mx(
+                    out=hidden[t, piece][:],
+                    lhsT=w_codes[g, t][:].bitcast(FP8X4),
+                    lhsT_scale=w_scales[g, t][:],
+                    rhs=x_codes[g][:, cols].bitcast(FP8X4),
+                    rhs_scale=x_scales[g][:, cols],
+                    start=first,
+                    stop=not first,
+                )
 
         for g in range(PASSES):
             dealt = sbuf("dealt%d" % g, [P, PACK, P, PACK], BF16, tag="staging%d" % (PASSES - 1))
-            source = w_raw[g][:].rearrange("p j (m t) -> p m j t", t=PACK)
-            target = dealt[:].rearrange("p t m j -> p m j t")
-            nc.vector.tensor_copy(out=target[:, :M_VECTOR], in_=source[:, :M_VECTOR])
-            nc.scalar.copy(out=target[:, M_VECTOR:], in_=source[:, M_VECTOR:])
+            for rows, loaded in w_raw[g]:
+                source = loaded[:].rearrange("p j (m t) -> p m j t", t=PACK)
+                target = dealt[:, :, :, rows].rearrange("p t m j -> p m j t")
+                nc.vector.tensor_copy(out=target[:, :M_VECTOR], in_=source[:, :M_VECTOR])
+                nc.scalar.copy(out=target[:, M_VECTOR:], in_=source[:, M_VECTOR:])
             for t in range(PACK):
-                w_codes = sbuf("w_codes%d%d" % (g, t), [P, P], U32)
-                w_scales = sbuf("w_scales%d%d" % (g, t), [P, P], U8)
+                w_codes[g, t] = sbuf("w_codes%d%d" % (g, t), [P, P], U32)
+                w_scales[g, t] = sbuf("w_scales%d%d" % (g, t), [P, P], U8)
                 nc.vector.quantize_mx(
-                    out=w_codes[:].bitcast(FP8X4),
-                    scales=w_scales[:],
+                    out=w_codes[g, t][:].bitcast(FP8X4),
+                    scales=w_scales[g, t][:],
                     in_=dealt[:, t].rearrange("p m j -> p (m j)"),
                 )
-                for piece, cols in enumerate(spans[t]):
-                    nc.tensor.matmul_mx(
-                        out=hidden[t, piece][:],
-                        lhsT=w_codes[:].bitcast(FP8X4),
-                        lhsT_scale=w_scales[:],
-                        rhs=x_codes[g][:, cols].bitcast(FP8X4),
-                        rhs_scale=x_scales[g][:, cols],
-                        start=(g == 0),
-                        stop=(g == PASSES - 1),
-                    )
+                if t < PACK - 1:
+                    project(g, t, first=(g == 0))
+        project(1, PACK - 1, first=True)
+        project(0, PACK - 1, first=False)
 
         z_planes = sbuf("z_planes", [P, PACK, S], BF16)
         affine = {}
@@ -125,25 +147,24 @@ def tile_picked_inorm_none_e_kernel(tc, xT, w1, w2_words, w2_scales, gamma, offs
                 affine[t][:], moments[t][:, 0:2], inv_std[t][:], neg_gain[:, t : t + 1], ALU.mult, ALU.mult
             )
 
-        first = sbuf("first", [P, S], F32)
+        evacuated = sbuf("evacuated", [P, S], F32)
         squares = sbuf("squares", [P, S], F32)
         sums = sbuf("sums", [P, 2], F32)
-        nc.scalar.activation(first[:], hidden[0, 0][:], ACT.Identity, accum_out=sums[:, 0:1])
-        nc.scalar.activation(moments[0][:, 1:2], sums[:, 0:1], ACT.Copy, scale=1.0 / S)
-        nc.scalar.activation(
-            squares[:], hidden[0, 0][:], ACT.Square, bias=moments[0][:, 1:2], scale=-1.0, accum_out=sums[:, 1:2]
-        )
-        inv_std[0] = sbuf("inv_std0", [P, 1], F32)
-        nc.scalar.activation(inv_std[0][:], sums[:, 1:2], ACT.Abs_reciprocal_sqrt, bias=EPS, scale=1.0 / S)
-        coefficients(0, nc.gpsimd)
-
-        for t in range(1, PACK):
-            for half in range(2):
-                nc.vector.bn_stats(partial[t][:, half, :], hidden[t, half][:])
-            nc.vector.bn_aggr(moments[t][:, 1:3], partial[t][:].rearrange("p h s -> p (h s)"))
+        for t in range(PACK):
             inv_std[t] = sbuf("inv_std%d" % t, [P, 1], F32)
-            nc.scalar.activation(inv_std[t][:], moments[t][:, 2:3], ACT.Abs_reciprocal_sqrt, bias=EPS)
-            coefficients(t, nc.gpsimd if t == 1 else nc.vector)
+            if t == SCALAR_PLANE:
+                nc.scalar.activation(evacuated[:], hidden[t, 0][:], ACT.Identity, accum_out=sums[:, 0:1])
+                nc.scalar.activation(moments[t][:, 1:2], sums[:, 0:1], ACT.Copy, scale=1.0 / S)
+                nc.scalar.activation(
+                    squares[:], hidden[t, 0][:], ACT.Square, bias=moments[t][:, 1:2], scale=-1.0, accum_out=sums[:, 1:2]
+                )
+                nc.scalar.activation(inv_std[t][:], sums[:, 1:2], ACT.Abs_reciprocal_sqrt, bias=EPS, scale=1.0 / S)
+            else:
+                for half in range(2):
+                    nc.vector.bn_stats(partial[t][:, half, :], hidden[t, half][:])
+                nc.vector.bn_aggr(moments[t][:, 1:3], partial[t][:].rearrange("p h s -> p (h s)"))
+                nc.scalar.activation(inv_std[t][:], moments[t][:, 2:3], ACT.Abs_reciprocal_sqrt, bias=EPS)
+            coefficients(t, nc.gpsimd if t == 0 else nc.vector)
 
         def normalise_vector(t, source, cols):
             nc.vector.tensor_scalar(
@@ -155,37 +176,39 @@ def tile_picked_inorm_none_e_kernel(tc, xT, w1, w2_words, w2_scales, gamma, offs
                 z_planes[:, t, cols], source, ACT.Identity, bias=affine[t][:, 1:2], scale=affine[t][:, 0:1]
             )
 
-        normalise_vector(0, first[:], slice(0, S))
-        for t in range(1, PACK):
+        for t in range(PACK):
             for half, cols in enumerate(spans[t]):
-                if (t, half) == (PACK - 1, 1):
+                if t == SCALAR_PLANE:
+                    normalise_vector(t, evacuated[:], cols)
+                elif t > SCALAR_PLANE and half == 1:
                     normalise_vector(t, hidden[t, half][:], cols)
                 else:
                     normalise_scalar(t, hidden[t, half][:], cols)
 
-        woven = [sbuf("woven%d" % half, [P, HALF, PACK], BF16) for half in range(2)]
+        chunks = S // CHUNK
+        woven = [sbuf("woven%d" % c, [P, CHUNK, PACK], BF16) for c in range(chunks)]
 
-        def weave(copy, half, start, stop):
+        def weave(copy, c):
             copy(
-                out=woven[half][:, start:stop, :].rearrange("p (c i) t -> p c t i", i=4),
-                in_=z_planes[:, :, half * HALF + start : half * HALF + stop].rearrange("p t (c i) -> p c t i", i=4),
+                out=woven[c][:].rearrange("p (c i) t -> p c t i", i=4),
+                in_=z_planes[:, :, c * CHUNK : (c + 1) * CHUNK].rearrange("p t (c i) -> p c t i", i=4),
             )
 
-        weave(nc.vector.tensor_copy, 0, 0, HALF)
-        weave(nc.vector.tensor_copy, 1, 0, HALF // 2)
-        weave(nc.scalar.copy, 1, HALF // 2, HALF)
-        out_rows = out.rearrange("(m p) s -> m p s", p=P)
-        for half in range(2):
-            cols = slice(half * HALF, (half + 1) * HALF)
-            z_codes = sbuf("z_codes%d" % half, [P, HALF], U32)
-            z_scales = sbuf("z_scales%d" % half, [P, HALF], U8)
+        for c in range(chunks):
+            weave(nc.vector.tensor_copy if c % 2 == 0 else nc.scalar.copy, c)
+        out_rows = out.rearrange("(m p) s -> p m s", p=P)
+        banks = ["bank%d%d" % key for key in hidden] + ["spare"]
+        for c in range(chunks):
+            z_codes = sbuf("z_codes%d" % c, [P, CHUNK], U32)
+            z_scales = sbuf("z_scales%d" % c, [P, CHUNK], U8)
             nc.vector.quantize_mx(
                 out=z_codes[:].bitcast(FP8X4),
                 scales=z_scales[:],
-                in_=woven[half][:].rearrange("p s t -> p (s t)"),
+                in_=woven[c][:].rearrange("p s t -> p (s t)"),
             )
+            result = sbuf("result%d" % c, [P, N // P, CHUNK], F32)
             for m in range(N // P):
-                acc = psum.tile([P, HALF], F32, name="acc%d%d" % (m, half), tag="bank%d%d" % (m + 1, half))
+                acc = psum.tile([P, CHUNK], F32, name="acc%d%d" % (m, c), tag=banks[2 * c + m])
                 nc.tensor.matmul_mx(
                     out=acc[:],
                     lhsT=w2_codes[:, 2 * P * m : 2 * P * (m + 1)].bitcast(FP4X4),
@@ -195,9 +218,8 @@ def tile_picked_inorm_none_e_kernel(tc, xT, w1, w2_words, w2_scales, gamma, offs
                     start=True,
                     stop=True,
                 )
-                result = sbuf("result%d%d" % (m, half), [P, HALF], F32)
-                if m == 1:
-                    nc.vector.tensor_copy(out=result[:], in_=acc[:])
+                if m == 1 and c >= 1:
+                    nc.vector.tensor_copy(out=result[:, m, :], in_=acc[:])
                 else:
-                    nc.scalar.copy(out=result[:], in_=acc[:])
-                nc.sync.dma_start(out=out_rows[m][:, cols], in_=result[:])
+                    nc.scalar.copy(out=result[:, m, :], in_=acc[:])
+            nc.sync.dma_start(out=out_rows[:, :, c * CHUNK : (c + 1) * CHUNK], in_=result[:])

@@ -23,6 +23,8 @@ PASSES = K // (P * PACK)
 HALF = S // 2
 M_VECTOR = 88
 CHUNK = 128
+X_LOADS = (((0, 2), (2, 2)), ((0, 1), (1, 1), (2, 1), (3, 1)))
+S_VECTOR = 344
 SCALAR_PLANE = 1
 
 
@@ -42,8 +44,7 @@ def tile_picked_inorm_none_e_kernel(tc, xT, w1, w2_words, w2_scales, gamma, offs
 
         x_planes = {}
         for g in range(PASSES):
-            rows_per_load = 2 if g == 0 else 1
-            for j0 in range(0, PACK, rows_per_load):
+            for j0, rows_per_load in X_LOADS[g]:
                 loaded = sbuf("x_rows%d%d" % (g, j0), [P, rows_per_load, T], F32)
                 nc.sync.dma_start(out=loaded[:], in_=x_rows[g][:, j0 : j0 + rows_per_load])
                 for j in range(rows_per_load):
@@ -52,7 +53,7 @@ def tile_picked_inorm_none_e_kernel(tc, xT, w1, w2_words, w2_scales, gamma, offs
                     nc.sync.dma_start(offsets[:], offs)
         w_raw = {}
         for g in range(PASSES):
-            rows_per_load = PACK if g == 0 else 2
+            rows_per_load = PACK
             w_raw[g] = []
             for j0 in range(0, PACK, rows_per_load):
                 loaded = sbuf("w_rows%d%d" % (g, j0), [P, rows_per_load, H], F32)
@@ -83,7 +84,18 @@ def tile_picked_inorm_none_e_kernel(tc, xT, w1, w2_words, w2_scales, gamma, offs
         x_codes, x_scales = [], []
         for g in range(PASSES):
             picked = sbuf("picked%d" % g, [P, S, PACK], BF16, tag="staging%d" % g)
-            for j in range(PACK):
+            woven_rows = PACK if g == 0 else 2
+            gathered = sbuf("gathered%d" % g, [P, woven_rows, S], F32)
+            for j in range(woven_rows):
+                nc.vector.tensor_copy(gathered[:, j, :], x_planes[g, j].indirect(offsets[:]))
+            split = S_VECTOR if g == 0 else 0
+            for copy, cols in ((nc.vector.tensor_copy, slice(0, split)), (nc.scalar.copy, slice(split, S))):
+                if cols.stop > cols.start:
+                    copy(
+                        out=picked[:, cols, :woven_rows].rearrange("p (c i) j -> p c j i", i=4),
+                        in_=gathered[:, :, cols].rearrange("p j (c i) -> p c j i", i=4),
+                    )
+            for j in range(woven_rows, PACK):
                 nc.vector.tensor_copy(picked[:, :, j], x_planes[g, j].indirect(offsets[:]))
             x_codes.append(sbuf("x_codes%d" % g, [P, S], U32))
             x_scales.append(sbuf("x_scales%d" % g, [P, S], U8))

@@ -21,7 +21,7 @@ P = 128
 PACK = 4
 PASSES = K // (P * PACK)
 HALF = S // 2
-M_VECTOR = 88
+M_VECTOR = (76, 88)
 CHUNK = 128
 X_LOADS = (((0, 2), (2, 2)), ((0, 1), (1, 1), (2, 1), (3, 1)))
 S_VECTOR = 344
@@ -83,7 +83,7 @@ def tile_picked_inorm_none_e_kernel(tc, xT, w1, w2_words, w2_scales, gamma, offs
 
         x_codes, x_scales = [], []
         for g in range(PASSES):
-            picked = sbuf("picked%d" % g, [P, S, PACK], BF16, tag="staging%d" % g)
+            picked = sbuf("picked%d" % g, [P, S, PACK], BF16)
             woven_rows = PACK if g == 0 else 2
             gathered = sbuf("gathered%d" % g, [P, woven_rows, S], F32)
             for j in range(woven_rows):
@@ -95,15 +95,19 @@ def tile_picked_inorm_none_e_kernel(tc, xT, w1, w2_words, w2_scales, gamma, offs
                         out=picked[:, cols, :woven_rows].rearrange("p (c i) j -> p c j i", i=4),
                         in_=gathered[:, :, cols].rearrange("p j (c i) -> p c j i", i=4),
                     )
+            halves = [slice(0, S)] if g == 0 else [slice(0, HALF), slice(HALF, S)]
             for j in range(woven_rows, PACK):
-                nc.vector.tensor_copy(picked[:, :, j], x_planes[g, j].indirect(offsets[:]))
+                for cols in halves if j == PACK - 1 else [slice(0, S)]:
+                    entries = offsets[:, cols.start // 16 : cols.stop // 16]
+                    nc.vector.tensor_copy(picked[:, cols, j], x_planes[g, j].indirect(entries))
             x_codes.append(sbuf("x_codes%d" % g, [P, S], U32))
             x_scales.append(sbuf("x_scales%d" % g, [P, S], U8))
-            nc.vector.quantize_mx(
-                out=x_codes[g][:].bitcast(FP8X4),
-                scales=x_scales[g][:],
-                in_=picked[:].rearrange("p s j -> p (s j)"),
-            )
+            for cols in halves:
+                nc.vector.quantize_mx(
+                    out=x_codes[g][:, cols].bitcast(FP8X4),
+                    scales=x_scales[g][:, cols],
+                    in_=picked[:, cols, :].rearrange("p s j -> p (s j)"),
+                )
 
         spans = {t: [slice(0, S)] if t == SCALAR_PLANE else [slice(0, HALF), slice(HALF, S)] for t in range(PACK)}
         hidden = {}
@@ -130,12 +134,12 @@ def tile_picked_inorm_none_e_kernel(tc, xT, w1, w2_words, w2_scales, gamma, offs
                 )
 
         for g in range(PASSES):
-            dealt = sbuf("dealt%d" % g, [P, PACK, P, PACK], BF16, tag="staging%d" % (PASSES - 1))
+            dealt = sbuf("dealt%d" % g, [P, PACK, P, PACK], BF16, tag="dealt")
             for rows, loaded in w_raw[g]:
                 source = loaded[:].rearrange("p j (m t) -> p m j t", t=PACK)
                 target = dealt[:, :, :, rows].rearrange("p t m j -> p m j t")
-                nc.vector.tensor_copy(out=target[:, :M_VECTOR], in_=source[:, :M_VECTOR])
-                nc.scalar.copy(out=target[:, M_VECTOR:], in_=source[:, M_VECTOR:])
+                nc.vector.tensor_copy(out=target[:, : M_VECTOR[g]], in_=source[:, : M_VECTOR[g]])
+                nc.scalar.copy(out=target[:, M_VECTOR[g] :], in_=source[:, M_VECTOR[g] :])
             for t in range(PACK):
                 w_codes[g, t] = sbuf("w_codes%d%d" % (g, t), [P, P], U32)
                 w_scales[g, t] = sbuf("w_scales%d%d" % (g, t), [P, P], U8)
@@ -234,4 +238,5 @@ def tile_picked_inorm_none_e_kernel(tc, xT, w1, w2_words, w2_scales, gamma, offs
                     nc.vector.tensor_copy(out=result[:, m, :], in_=acc[:])
                 else:
                     nc.scalar.copy(out=result[:, m, :], in_=acc[:])
-            nc.sync.dma_start(out=out_rows[:, :, c * CHUNK : (c + 1) * CHUNK], in_=result[:])
+            for rows in [slice(0, 2)] if c < chunks - 1 else [slice(0, 1), slice(1, 2)]:
+                nc.sync.dma_start(out=out_rows[:, rows, c * CHUNK : (c + 1) * CHUNK], in_=result[:, rows, :])

@@ -21,10 +21,9 @@ P = 128
 PACK = 4
 PASSES = K // (P * PACK)
 HALF = S // 2
-M_VECTOR = (76, 88)
 CHUNK = 128
-X_LOADS = (((0, 2), (2, 2)), ((0, 1), (1, 1), (2, 1), (3, 1)))
-S_VECTOR = 344
+M_HALF = P // 2
+W_PIECES = ((0, 0, P, 84), (1, 0, M_HALF, 24), (1, M_HALF, P, 42))
 SCALAR_PLANE = 1
 
 
@@ -43,22 +42,28 @@ def tile_picked_inorm_none_e_kernel(tc, xT, w1, w2_words, w2_scales, gamma, offs
         w_rows = w1.rearrange("(g p j) c -> g p j c", p=P, j=PACK)
 
         x_planes = {}
-        for g in range(PASSES):
-            for j0, rows_per_load in X_LOADS[g]:
-                loaded = sbuf("x_rows%d%d" % (g, j0), [P, rows_per_load, T], F32)
-                nc.sync.dma_start(out=loaded[:], in_=x_rows[g][:, j0 : j0 + rows_per_load])
-                for j in range(rows_per_load):
-                    x_planes[g, j0 + j] = loaded[:, j, :]
-                if (g, j0) == (0, 0):
-                    nc.sync.dma_start(offsets[:], offs)
         w_raw = {}
-        for g in range(PASSES):
-            rows_per_load = PACK
-            w_raw[g] = []
-            for j0 in range(0, PACK, rows_per_load):
-                loaded = sbuf("w_rows%d%d" % (g, j0), [P, rows_per_load, H], F32)
-                nc.sync.dma_start(out=loaded[:], in_=w_rows[g][:, j0 : j0 + rows_per_load])
-                w_raw[g].append((slice(j0, j0 + rows_per_load), loaded))
+
+        def load_x(g, j0, rows):
+            loaded = sbuf("x_rows%d%d" % (g, j0), [P, rows, T], F32)
+            nc.sync.dma_start(out=loaded[:], in_=x_rows[g][:, j0 : j0 + rows])
+            for j in range(rows):
+                x_planes[g, j0 + j] = loaded[:, j, :]
+
+        def load_w(g, m0, m1):
+            w_raw[g, m0] = sbuf("w_rows%d%d" % (g, m0), [P, PACK, PACK * (m1 - m0)], F32)
+            nc.sync.dma_start(out=w_raw[g, m0][:], in_=w_rows[g][:, :, PACK * m0 : PACK * m1])
+
+        load_x(0, 0, 2)
+        nc.sync.dma_start(offsets[:], offs)
+        load_x(0, 2, 2)
+        load_x(1, 0, 1)
+        load_x(1, 1, 1)
+        load_x(1, 2, 1)
+        load_x(1, 3, 1)
+        load_w(0, 0, P)
+        load_w(1, 0, M_HALF)
+        load_w(1, M_HALF, P)
         nc.sync.dma_start(out=gain[:], in_=gamma.rearrange("(p t) o -> p (t o)", t=PACK))
         w2_codes = sbuf("w2_codes", [P, 2 * N], U8)
         nc.sync.dma_start(out=w2_codes[:].bitcast(I32), in_=w2_words[0].bitcast(I32))
@@ -78,36 +83,52 @@ def tile_picked_inorm_none_e_kernel(tc, xT, w1, w2_words, w2_scales, gamma, offs
         nc.gpsimd.tensor_scalar(neg_gain[:], gain[:], -1.0, 0.0, ALU.mult, ALU.add)
         moments = []
         for t in range(PACK):
-            moments.append(sbuf("moments%d" % t, [P, 3], F32))
-            nc.vector.memset(moments[t][:, 0:1], -1.0)
+            moments.append(sbuf("moments%d" % t, [P, 4], F32))
+            nc.vector.memset(moments[t][:, 0:1], -float(S if t == SCALAR_PLANE else HALF))
+            nc.vector.memset(moments[t][:, 1:2], -1.0)
 
-        x_codes, x_scales = [], []
-        for g in range(PASSES):
-            picked = sbuf("picked%d" % g, [P, S, PACK], BF16)
-            woven_rows = PACK if g == 0 else 2
-            gathered = sbuf("gathered%d" % g, [P, woven_rows, S], F32)
-            for j in range(woven_rows):
-                nc.vector.tensor_copy(gathered[:, j, :], x_planes[g, j].indirect(offsets[:]))
-            split = S_VECTOR if g == 0 else 0
-            for copy, cols in ((nc.vector.tensor_copy, slice(0, split)), (nc.scalar.copy, slice(split, S))):
-                if cols.stop > cols.start:
-                    copy(
-                        out=picked[:, cols, :woven_rows].rearrange("p (c i) j -> p c j i", i=4),
-                        in_=gathered[:, :, cols].rearrange("p j (c i) -> p c j i", i=4),
-                    )
-            halves = [slice(0, S)] if g == 0 else [slice(0, HALF), slice(HALF, S)]
-            for j in range(woven_rows, PACK):
-                for cols in halves if j == PACK - 1 else [slice(0, S)]:
-                    entries = offsets[:, cols.start // 16 : cols.stop // 16]
-                    nc.vector.tensor_copy(picked[:, cols, j], x_planes[g, j].indirect(entries))
-            x_codes.append(sbuf("x_codes%d" % g, [P, S], U32))
-            x_scales.append(sbuf("x_scales%d" % g, [P, S], U8))
-            for cols in halves:
-                nc.vector.quantize_mx(
-                    out=x_codes[g][:, cols].bitcast(FP8X4),
-                    scales=x_scales[g][:, cols],
-                    in_=picked[:, cols, :].rearrange("p s j -> p (s j)"),
-                )
+        halves = [slice(0, HALF), slice(HALF, S)]
+        x_codes = [sbuf("x_codes%d" % g, [P, S], U32) for g in range(PASSES)]
+        x_scales = [sbuf("x_scales%d" % g, [P, S], U8) for g in range(PASSES)]
+
+        def gather(target, g, j, cols):
+            entries = offsets[:, cols.start // 16 : cols.stop // 16]
+            nc.vector.tensor_copy(target, x_planes[g, j].indirect(entries))
+
+        def weave_x(copy, target, source):
+            copy(
+                out=target.rearrange("p (c i) j -> p c j i", i=4),
+                in_=source.rearrange("p j (c i) -> p c j i", i=4),
+            )
+
+        def quantise_x(g, cols, source):
+            nc.vector.quantize_mx(
+                out=x_codes[g][:, cols].bitcast(FP8X4),
+                scales=x_scales[g][:, cols],
+                in_=source.rearrange("p s j -> p (s j)"),
+            )
+
+        everything = slice(0, S)
+        first_rows = sbuf("first_rows", [P, PACK, S], F32)
+        first_picked = sbuf("first_picked", [P, S, PACK], BF16)
+        for j in range(PACK):
+            gather(first_rows[:, j, :], 0, j, everything)
+        weave_x(nc.vector.tensor_copy, first_picked[:, :HALF], first_rows[:, :, :HALF])
+        weave_x(nc.scalar.copy, first_picked[:, HALF:], first_rows[:, :, HALF:])
+        early_rows = sbuf("early_rows", [P, 2, S], F32)
+        for j in range(2):
+            gather(early_rows[:, j, :], 1, j, everything)
+        quantise_x(0, everything, first_picked[:])
+        last_picked = [sbuf("last_picked%d" % h, [P, HALF, PACK], BF16) for h in range(2)]
+        late_rows = sbuf("late_rows", [P, 2, HALF], F32)
+        for h, cols in enumerate(halves):
+            weave_x(nc.scalar.copy, last_picked[h][:, :, 0:2], early_rows[:, :, cols])
+        for j in (2, 3):
+            gather(late_rows[:, j - 2, :], 1, j, halves[0])
+            gather(last_picked[1][:, :, j], 1, j, halves[1])
+        weave_x(nc.scalar.copy, last_picked[0][:, :, 2:4], late_rows[:])
+        for h in (1, 0):
+            quantise_x(1, halves[h], last_picked[h][:])
 
         spans = {t: [slice(0, S)] if t == SCALAR_PLANE else [slice(0, HALF), slice(HALF, S)] for t in range(PACK)}
         hidden = {}
@@ -117,7 +138,8 @@ def tile_picked_inorm_none_e_kernel(tc, xT, w1, w2_words, w2_scales, gamma, offs
                     [P, cols.stop - cols.start], F32, name="hidden%d%d" % (t, piece), tag="bank%d%d" % (t, piece)
                 )
 
-        partial = {t: sbuf("partial%d" % t, [P, 2, 6], F32) for t in range(PACK) if t != SCALAR_PLANE}
+        partial = {t: sbuf("partial%d" % t, [P, 9 if t == 0 else 12], F32) for t in range(PACK) if t != SCALAR_PLANE}
+        nc.vector.memset(partial[0][:, 6:7], float(HALF))
 
         w_codes, w_scales = {}, {}
 
@@ -134,87 +156,127 @@ def tile_picked_inorm_none_e_kernel(tc, xT, w1, w2_words, w2_scales, gamma, offs
                 )
 
         for g in range(PASSES):
-            dealt = sbuf("dealt%d" % g, [P, PACK, P, PACK], BF16, tag="dealt")
-            for rows, loaded in w_raw[g]:
-                source = loaded[:].rearrange("p j (m t) -> p m j t", t=PACK)
-                target = dealt[:, :, :, rows].rearrange("p t m j -> p m j t")
-                nc.vector.tensor_copy(out=target[:, : M_VECTOR[g]], in_=source[:, : M_VECTOR[g]])
-                nc.scalar.copy(out=target[:, M_VECTOR[g] :], in_=source[:, M_VECTOR[g] :])
             for t in range(PACK):
                 w_codes[g, t] = sbuf("w_codes%d%d" % (g, t), [P, P], U32)
                 w_scales[g, t] = sbuf("w_scales%d%d" % (g, t), [P, P], U8)
-                nc.vector.quantize_mx(
-                    out=w_codes[g, t][:].bitcast(FP8X4),
-                    scales=w_scales[g, t][:],
-                    in_=dealt[:, t].rearrange("p m j -> p (m j)"),
-                )
-                if t < PACK - 1:
-                    project(g, t, first=(g == 0))
-        project(1, PACK - 1, first=True)
-        project(0, PACK - 1, first=False)
+        dealt = [sbuf("dealt%d" % g, [P, PACK, P, PACK], BF16) for g in range(PASSES)]
+
+        def deal(g, m0, m1, vector_share):
+            source = w_raw[g, m0][:].rearrange("p j (m t) -> p m j t", t=PACK)
+            target = dealt[g][:, :, m0:m1, :].rearrange("p t m j -> p m j t")
+            nc.vector.tensor_copy(out=target[:, :vector_share], in_=source[:, :vector_share])
+            nc.scalar.copy(out=target[:, vector_share:], in_=source[:, vector_share:])
+
+        def quantise_w(g, t):
+            nc.vector.quantize_mx(
+                out=w_codes[g, t][:].bitcast(FP8X4),
+                scales=w_scales[g, t][:],
+                in_=dealt[g][:, t].rearrange("p m j -> p (m j)"),
+            )
+
+        unread = psum.tile([P, S], F32, name="unread", tag="spare")
+        for first in (True, False):
+            nc.tensor.matmul_mx(
+                out=unread[:],
+                lhsT=x_codes[1][:, S - P :].bitcast(FP8X4),
+                lhsT_scale=x_scales[1][:, S - P :],
+                rhs=x_codes[0][:].bitcast(FP8X4),
+                rhs_scale=x_scales[0][:],
+                start=first,
+                stop=not first,
+            )
+        deal(*W_PIECES[0])
+        for t in range(PACK):
+            quantise_w(0, t)
+            project(0, t, first=True)
+        deal(*W_PIECES[1])
+        deal(*W_PIECES[2])
+        for t in range(PACK):
+            quantise_w(1, t)
+            project(1, t, first=False)
 
         z_planes = sbuf("z_planes", [P, PACK, S], BF16)
         affine = {}
         inv_std = {}
 
-        def coefficients(t, engine):
-            affine[t] = sbuf("affine%d" % t, [P, 2], F32)
-            engine.tensor_scalar(
-                affine[t][:], moments[t][:, 0:2], inv_std[t][:], neg_gain[:, t : t + 1], ALU.mult, ALU.mult
+        def coefficients(t):
+            affine[t] = sbuf("affine%d" % t, [P, 3], F32)
+            nc.vector.tensor_scalar(
+                affine[t][:], moments[t][:, 0:3], inv_std[t][:], neg_gain[:, t : t + 1], ALU.mult, ALU.mult
             )
 
-        evacuated = sbuf("evacuated", [P, S], F32)
-        squares = sbuf("squares", [P, S], F32)
-        sums = sbuf("sums", [P, 2], F32)
+        evacuated = {(0, 0): sbuf("evacuated0", [P, HALF], F32), (1, 0): sbuf("evacuated1", [P, S], F32)}
+        squares = sbuf("squares", [P, S + HALF], F32)
+        mean_at = {(0, 0): partial[0][:, 7:8], (1, 0): moments[1][:, 2:3]}
+        spread_at = {(0, 0): partial[0][:, 8:9], (1, 0): moments[1][:, 3:4]}
+        for key, copy in evacuated.items():
+            nc.scalar.activation(copy[:], hidden[key][:], ACT.Identity, scale=1.0 / copy.shape[1], accum_out=mean_at[key])
+        for key, copy in evacuated.items():
+            nc.scalar.activation(
+                squares[:, HALF * key[0] : HALF * key[0] + copy.shape[1]],
+                hidden[key][:],
+                ACT.Square,
+                bias=mean_at[key],
+                scale=-1.0,
+                accum_out=spread_at[key],
+            )
         for t in range(PACK):
             inv_std[t] = sbuf("inv_std%d" % t, [P, 1], F32)
+            for half in range(len(spans[t])):
+                if (t, half) not in evacuated:
+                    at = 0 if t == 0 else 6 * half
+                    nc.vector.bn_stats(partial[t][:, at : at + 6], hidden[t, half][:])
             if t == SCALAR_PLANE:
-                nc.scalar.activation(evacuated[:], hidden[t, 0][:], ACT.Identity, accum_out=sums[:, 0:1])
-                nc.scalar.activation(moments[t][:, 1:2], sums[:, 0:1], ACT.Copy, scale=1.0 / S)
-                nc.scalar.activation(
-                    squares[:], hidden[t, 0][:], ACT.Square, bias=moments[t][:, 1:2], scale=-1.0, accum_out=sums[:, 1:2]
-                )
-                nc.scalar.activation(inv_std[t][:], sums[:, 1:2], ACT.Abs_reciprocal_sqrt, bias=EPS, scale=1.0 / S)
+                nc.scalar.activation(inv_std[t][:], moments[t][:, 3:4], ACT.Abs_reciprocal_sqrt, bias=EPS, scale=1.0 / S)
             else:
-                for half in range(2):
-                    nc.vector.bn_stats(partial[t][:, half, :], hidden[t, half][:])
-                nc.vector.bn_aggr(moments[t][:, 1:3], partial[t][:].rearrange("p h s -> p (h s)"))
-                nc.scalar.activation(inv_std[t][:], moments[t][:, 2:3], ACT.Abs_reciprocal_sqrt, bias=EPS)
-            coefficients(t, nc.gpsimd if t == 0 else nc.vector)
+                nc.vector.bn_aggr(moments[t][:, 2:4], partial[t][:])
+                nc.scalar.activation(inv_std[t][:], moments[t][:, 3:4], ACT.Abs_reciprocal_sqrt, bias=EPS)
+            coefficients(t)
 
-        def normalise_vector(t, source, cols):
-            nc.vector.tensor_scalar(
-                z_planes[:, t, cols], source, affine[t][:, 0:1], affine[t][:, 1:2], ALU.mult, ALU.add
-            )
-
-        def normalise_scalar(t, source, cols):
-            nc.scalar.activation(
-                z_planes[:, t, cols], source, ACT.Identity, bias=affine[t][:, 1:2], scale=affine[t][:, 0:1]
-            )
-
-        for t in range(PACK):
-            for half, cols in enumerate(spans[t]):
-                if t == SCALAR_PLANE:
-                    normalise_vector(t, evacuated[:], cols)
-                elif t > SCALAR_PLANE and half == 1:
-                    normalise_vector(t, hidden[t, half][:], cols)
-                else:
-                    normalise_scalar(t, hidden[t, half][:], cols)
+        for t, half in hidden:
+            target = z_planes[:, t, spans[t][half]]
+            if (t, half) in evacuated:
+                nc.vector.tensor_scalar(
+                    target, evacuated[t, half][:], affine[t][:, 0:1], affine[t][:, 2:3], ALU.mult, ALU.add
+                )
+            elif t > 1 and half == 1:
+                nc.vector.tensor_scalar(
+                    target, hidden[t, half][:], affine[t][:, 1:2], affine[t][:, 2:3], ALU.mult, ALU.add
+                )
+            else:
+                nc.scalar.activation(
+                    target, hidden[t, half][:], ACT.Identity, bias=affine[t][:, 2:3], scale=affine[t][:, 1:2]
+                )
 
         chunks = S // CHUNK
         woven = [sbuf("woven%d" % c, [P, CHUNK, PACK], BF16) for c in range(chunks)]
 
-        def weave(copy, c):
+        def weave(copy, c, s0, s1):
             copy(
-                out=woven[c][:].rearrange("p (c i) t -> p c t i", i=4),
-                in_=z_planes[:, :, c * CHUNK : (c + 1) * CHUNK].rearrange("p t (c i) -> p c t i", i=4),
+                out=woven[c][:, s0:s1, :].rearrange("p (c i) t -> p c t i", i=4),
+                in_=z_planes[:, :, c * CHUNK + s0 : c * CHUNK + s1].rearrange("p t (c i) -> p c t i", i=4),
             )
 
-        for c in range(chunks):
-            weave(nc.vector.tensor_copy if c % 2 == 0 else nc.scalar.copy, c)
+        weave(nc.vector.tensor_copy, 0, 0, CHUNK)
+        weave(nc.scalar.copy, 1, 0, CHUNK)
+        weave(nc.vector.tensor_copy, 2, 0, CHUNK)
+        weave(nc.vector.tensor_copy, 3, 0, CHUNK // 2)
+        weave(nc.scalar.copy, 3, CHUNK // 2, CHUNK)
         out_rows = out.rearrange("(m p) s -> p m s", p=P)
-        banks = ["bank%d%d" % key for key in hidden] + ["spare"]
-        for c in range(chunks):
+        banks = ["spare"] + ["bank%d%d" % key for key in hidden]
+
+        def second_product(acc, m, z_codes, z_scales):
+            nc.tensor.matmul_mx(
+                out=acc,
+                lhsT=w2_codes[:, 2 * P * m : 2 * P * (m + 1)].bitcast(FP4X4),
+                lhsT_scale=w2_plane[:, P * m : P * (m + 1)],
+                rhs=z_codes[:].bitcast(FP8X4),
+                rhs_scale=z_scales[:],
+                start=True,
+                stop=True,
+            )
+
+        for c in (0, 2, 1, 3):
             z_codes = sbuf("z_codes%d" % c, [P, CHUNK], U32)
             z_scales = sbuf("z_scales%d" % c, [P, CHUNK], U8)
             nc.vector.quantize_mx(
@@ -223,20 +285,16 @@ def tile_picked_inorm_none_e_kernel(tc, xT, w1, w2_words, w2_scales, gamma, offs
                 in_=woven[c][:].rearrange("p s t -> p (s t)"),
             )
             result = sbuf("result%d" % c, [P, N // P, CHUNK], F32)
-            for m in range(N // P):
-                acc = psum.tile([P, CHUNK], F32, name="acc%d%d" % (m, c), tag=banks[2 * c + m])
-                nc.tensor.matmul_mx(
-                    out=acc[:],
-                    lhsT=w2_codes[:, 2 * P * m : 2 * P * (m + 1)].bitcast(FP4X4),
-                    lhsT_scale=w2_plane[:, P * m : P * (m + 1)],
-                    rhs=z_codes[:].bitcast(FP8X4),
-                    rhs_scale=z_scales[:],
-                    start=True,
-                    stop=True,
-                )
-                if m == 1 and c >= 1:
-                    nc.vector.tensor_copy(out=result[:, m, :], in_=acc[:])
-                else:
-                    nc.scalar.copy(out=result[:, m, :], in_=acc[:])
-            for rows in [slice(0, 2)] if c < chunks - 1 else [slice(0, 1), slice(1, 2)]:
-                nc.sync.dma_start(out=out_rows[:, rows, c * CHUNK : (c + 1) * CHUNK], in_=result[:, rows, :])
+            cols = slice(c * CHUNK, (c + 1) * CHUNK)
+            if c < chunks - 1:
+                acc = psum.tile([P, N // P, CHUNK], F32, name="acc%d" % c, tag=banks[c])
+                for m in range(N // P):
+                    second_product(acc[:, m, :], m, z_codes, z_scales)
+                (nc.vector.tensor_copy if c == 1 else nc.scalar.copy)(out=result[:], in_=acc[:])
+                nc.sync.dma_start(out=out_rows[:, :, cols], in_=result[:])
+            else:
+                for m, copy in enumerate((nc.scalar.copy, nc.vector.tensor_copy)):
+                    acc = psum.tile([P, CHUNK], F32, name="acc%d%d" % (c, m), tag=banks[c + m])
+                    second_product(acc[:], m, z_codes, z_scales)
+                    copy(out=result[:, m, :], in_=acc[:])
+                    nc.sync.dma_start(out=out_rows[:, m, cols], in_=result[:, m, :])

@@ -161,9 +161,9 @@ def tile_picked_inorm_none_e_kernel(tc, xT, w1, w2_words, w2_scales, gamma, offs
                 w_scales[g, t] = sbuf("w_scales%d%d" % (g, t), [P, P], U8)
         dealt = [sbuf("dealt%d" % g, [P, PACK, P, PACK], BF16) for g in range(PASSES)]
 
-        def deal(g, m0, m1, vector_share):
-            source = w_raw[g, m0][:].rearrange("p j (m t) -> p m j t", t=PACK)
-            target = dealt[g][:, :, m0:m1, :].rearrange("p t m j -> p m j t")
+        def deal(g, m0, m1, vector_share, planes=slice(0, PACK)):
+            source = w_raw[g, m0][:].rearrange("p j (m t) -> p m j t", t=PACK)[:, :, :, planes]
+            target = dealt[g][:, planes, m0:m1, :].rearrange("p t m j -> p m j t")
             nc.vector.tensor_copy(out=target[:, :vector_share], in_=source[:, :vector_share])
             nc.scalar.copy(out=target[:, vector_share:], in_=source[:, vector_share:])
 
@@ -190,7 +190,8 @@ def tile_picked_inorm_none_e_kernel(tc, xT, w1, w2_words, w2_scales, gamma, offs
             quantise_w(0, t)
             project(0, t, first=True)
         deal(*W_PIECES[1])
-        deal(*W_PIECES[2])
+        deal(*W_PIECES[2], planes=slice(0, 2))
+        deal(*W_PIECES[2], planes=slice(2, PACK))
         for t in range(PACK):
             quantise_w(1, t)
             project(1, t, first=False)
@@ -233,20 +234,27 @@ def tile_picked_inorm_none_e_kernel(tc, xT, w1, w2_words, w2_scales, gamma, offs
                 nc.scalar.activation(inv_std[t][:], moments[t][:, 3:4], ACT.Abs_reciprocal_sqrt, bias=EPS)
             coefficients(t)
 
+        def normalise_vector(t, source, cols, factor):
+            nc.vector.tensor_scalar(
+                z_planes[:, t, cols], source, affine[t][:, factor : factor + 1], affine[t][:, 2:3], ALU.mult, ALU.add
+            )
+
         for t, half in hidden:
-            target = z_planes[:, t, spans[t][half]]
+            cols = spans[t][half]
             if (t, half) in evacuated:
-                nc.vector.tensor_scalar(
-                    target, evacuated[t, half][:], affine[t][:, 0:1], affine[t][:, 2:3], ALU.mult, ALU.add
-                )
-            elif t > 1 and half == 1:
-                nc.vector.tensor_scalar(
-                    target, hidden[t, half][:], affine[t][:, 1:2], affine[t][:, 2:3], ALU.mult, ALU.add
-                )
+                normalise_vector(t, evacuated[t, half][:, :HALF], halves[0], 0)
+            elif (t, half) == (2, 0):
+                normalise_vector(t, hidden[t, half][:], cols, 1)
+            elif (t, half) == (3, 0):
+                for c in range(2):
+                    part = slice(c * CHUNK, (c + 1) * CHUNK)
+                    normalise_vector(t, hidden[t, half][:, part], part, 1)
             else:
                 nc.scalar.activation(
-                    target, hidden[t, half][:], ACT.Identity, bias=affine[t][:, 2:3], scale=affine[t][:, 1:2]
+                    z_planes[:, t, cols], hidden[t, half][:], ACT.Identity, bias=affine[t][:, 2:3], scale=affine[t][:, 1:2]
                 )
+
+        normalise_vector(SCALAR_PLANE, evacuated[SCALAR_PLANE, 0][:, HALF:], halves[1], 0)
 
         chunks = S // CHUNK
         woven = [sbuf("woven%d" % c, [P, CHUNK, PACK], BF16) for c in range(chunks)]
@@ -257,11 +265,6 @@ def tile_picked_inorm_none_e_kernel(tc, xT, w1, w2_words, w2_scales, gamma, offs
                 in_=z_planes[:, :, c * CHUNK + s0 : c * CHUNK + s1].rearrange("p t (c i) -> p c t i", i=4),
             )
 
-        weave(nc.vector.tensor_copy, 0, 0, CHUNK)
-        weave(nc.scalar.copy, 1, 0, CHUNK)
-        weave(nc.vector.tensor_copy, 2, 0, CHUNK)
-        weave(nc.vector.tensor_copy, 3, 0, CHUNK // 2)
-        weave(nc.scalar.copy, 3, CHUNK // 2, CHUNK)
         out_rows = out.rearrange("(m p) s -> p m s", p=P)
         banks = ["spare"] + ["bank%d%d" % key for key in hidden]
 
@@ -276,7 +279,7 @@ def tile_picked_inorm_none_e_kernel(tc, xT, w1, w2_words, w2_scales, gamma, offs
                 stop=True,
             )
 
-        for c in (0, 2, 1, 3):
+        def quantise_z(c):
             z_codes = sbuf("z_codes%d" % c, [P, CHUNK], U32)
             z_scales = sbuf("z_scales%d" % c, [P, CHUNK], U8)
             nc.vector.quantize_mx(
@@ -284,17 +287,25 @@ def tile_picked_inorm_none_e_kernel(tc, xT, w1, w2_words, w2_scales, gamma, offs
                 scales=z_scales[:],
                 in_=woven[c][:].rearrange("p s t -> p (s t)"),
             )
+            return z_codes, z_scales
+
+        def second_layer(c, copies):
             result = sbuf("result%d" % c, [P, N // P, CHUNK], F32)
-            cols = slice(c * CHUNK, (c + 1) * CHUNK)
-            if c < chunks - 1:
-                acc = psum.tile([P, N // P, CHUNK], F32, name="acc%d" % c, tag=banks[c])
-                for m in range(N // P):
-                    second_product(acc[:, m, :], m, z_codes, z_scales)
-                (nc.vector.tensor_copy if c == 1 else nc.scalar.copy)(out=result[:], in_=acc[:])
-                nc.sync.dma_start(out=out_rows[:, :, cols], in_=result[:])
-            else:
-                for m, copy in enumerate((nc.scalar.copy, nc.vector.tensor_copy)):
-                    acc = psum.tile([P, CHUNK], F32, name="acc%d%d" % (c, m), tag=banks[c + m])
-                    second_product(acc[:], m, z_codes, z_scales)
-                    copy(out=result[:, m, :], in_=acc[:])
-                    nc.sync.dma_start(out=out_rows[:, m, cols], in_=result[:, m, :])
+            for m, copy in enumerate(copies):
+                acc = psum.tile([P, CHUNK], F32, name="acc%d%d" % (c, m), tag=banks[2 * c + m])
+                second_product(acc[:], m, *codes[c])
+                copy(out=result[:, m, :], in_=acc[:])
+            for rows in [slice(0, 2)] if c < chunks - 1 else [slice(0, 1), slice(1, 2)]:
+                nc.sync.dma_start(out=out_rows[:, rows, c * CHUNK : (c + 1) * CHUNK], in_=result[:, rows, :])
+
+        weave(nc.vector.tensor_copy, 0, 0, CHUNK)
+        weave(nc.scalar.copy, 2, 0, CHUNK)
+        weave(nc.scalar.copy, 3, 0, CHUNK // 2)
+        codes = [quantise_z(0)]
+        weave(nc.vector.tensor_copy, 1, 0, CHUNK)
+        codes.append(quantise_z(1))
+        weave(nc.vector.tensor_copy, 3, CHUNK // 2, CHUNK)
+        codes.extend(quantise_z(c) for c in (2, 3))
+        second_layer(0, [nc.scalar.copy, nc.scalar.copy])
+        for c in range(1, chunks):
+            second_layer(c, [nc.scalar.copy, nc.vector.tensor_copy])

@@ -23,7 +23,7 @@ PASSES = K // (P * PACK)
 HALF = S // 2
 CHUNK = 128
 M_HALF = P // 2
-W_PIECES = ((0, 0, P, 84), (1, 0, M_HALF, 24), (1, M_HALF, P, 42))
+W_PIECES = ((0, 0, P, 72), (1, 0, M_HALF, 12), (1, M_HALF, P, 42))
 SCALAR_PLANE = 1
 
 
@@ -141,24 +141,20 @@ def tile_picked_inorm_none_e_kernel(tc, xT, w1, w2_words, w2_scales, gamma, offs
         partial = {t: sbuf("partial%d" % t, [P, 9 if t == 0 else 12], F32) for t in range(PACK) if t != SCALAR_PLANE}
         nc.vector.memset(partial[0][:, 6:7], float(HALF))
 
-        w_codes, w_scales = {}, {}
-
         def project(g, t, first):
             for piece, cols in enumerate(spans[t]):
                 nc.tensor.matmul_mx(
                     out=hidden[t, piece][:],
-                    lhsT=w_codes[g, t][:].bitcast(FP8X4),
-                    lhsT_scale=w_scales[g, t][:],
+                    lhsT=w_codes[g][:, P * t : P * (t + 1)].bitcast(FP8X4),
+                    lhsT_scale=w_scales[g][:, P * t : P * (t + 1)],
                     rhs=x_codes[g][:, cols].bitcast(FP8X4),
                     rhs_scale=x_scales[g][:, cols],
                     start=first,
                     stop=not first,
                 )
 
-        for g in range(PASSES):
-            for t in range(PACK):
-                w_codes[g, t] = sbuf("w_codes%d%d" % (g, t), [P, P], U32)
-                w_scales[g, t] = sbuf("w_scales%d%d" % (g, t), [P, P], U8)
+        w_codes = [sbuf("w_codes%d" % g, [P, H], U32) for g in range(PASSES)]
+        w_scales = [sbuf("w_scales%d" % g, [P, H], U8) for g in range(PASSES)]
         dealt = [sbuf("dealt%d" % g, [P, PACK, P, PACK], BF16) for g in range(PASSES)]
 
         def deal(g, m0, m1, vector_share, planes=slice(0, PACK)):
@@ -167,11 +163,11 @@ def tile_picked_inorm_none_e_kernel(tc, xT, w1, w2_words, w2_scales, gamma, offs
             nc.vector.tensor_copy(out=target[:, :vector_share], in_=source[:, :vector_share])
             nc.scalar.copy(out=target[:, vector_share:], in_=source[:, vector_share:])
 
-        def quantise_w(g, t):
+        def quantise_w(g, t0, t1):
             nc.vector.quantize_mx(
-                out=w_codes[g, t][:].bitcast(FP8X4),
-                scales=w_scales[g, t][:],
-                in_=dealt[g][:, t].rearrange("p m j -> p (m j)"),
+                out=w_codes[g][:, P * t0 : P * t1].bitcast(FP8X4),
+                scales=w_scales[g][:, P * t0 : P * t1],
+                in_=dealt[g][:, t0:t1].rearrange("p t m j -> p (t m j)"),
             )
 
         unread = psum.tile([P, S], F32, name="unread", tag="spare")
@@ -186,14 +182,15 @@ def tile_picked_inorm_none_e_kernel(tc, xT, w1, w2_words, w2_scales, gamma, offs
                 stop=not first,
             )
         deal(*W_PIECES[0])
-        for t in range(PACK):
-            quantise_w(0, t)
+        for t in range(0, PACK, 2):
+            quantise_w(0, t, t + 2)
             project(0, t, first=True)
+            project(0, t + 1, first=True)
         deal(*W_PIECES[1])
         deal(*W_PIECES[2], planes=slice(0, 2))
         deal(*W_PIECES[2], planes=slice(2, PACK))
         for t in range(PACK):
-            quantise_w(1, t)
+            quantise_w(1, t, t + 1)
             project(1, t, first=False)
 
         z_planes = sbuf("z_planes", [P, PACK, S], BF16)

@@ -23,8 +23,9 @@ PASSES = K // (P * PACK)
 HALF = S // 2
 CHUNK = 128
 M_HALF = P // 2
-W_PIECES = ((0, 0, P, 72), (1, 0, M_HALF, 12), (1, M_HALF, P, 42))
+W_PIECES = ((0, 0, P, 76), (1, 0, M_HALF, 16), (1, M_HALF, P, 42))
 SCALAR_PLANE = 1
+LATE_VECTOR = (84, 152)
 
 
 def tile_picked_inorm_none_e_kernel(tc, xT, w1, w2_words, w2_scales, gamma, offs, out):
@@ -57,8 +58,7 @@ def tile_picked_inorm_none_e_kernel(tc, xT, w1, w2_words, w2_scales, gamma, offs
         load_x(0, 0, 2)
         nc.sync.dma_start(offsets[:], offs)
         load_x(0, 2, 2)
-        load_x(1, 0, 1)
-        load_x(1, 1, 1)
+        load_x(1, 0, 2)
         load_x(1, 2, 1)
         load_x(1, 3, 1)
         load_w(0, 0, P)
@@ -120,15 +120,17 @@ def tile_picked_inorm_none_e_kernel(tc, xT, w1, w2_words, w2_scales, gamma, offs
             gather(early_rows[:, j, :], 1, j, everything)
         quantise_x(0, everything, first_picked[:])
         last_picked = [sbuf("last_picked%d" % h, [P, HALF, PACK], BF16) for h in range(2)]
-        late_rows = sbuf("late_rows", [P, 2, HALF], F32)
+        late_rows = [sbuf("late_rows%d" % h, [P, 2, HALF], F32) for h in range(2)]
         for h, cols in enumerate(halves):
             weave_x(nc.scalar.copy, last_picked[h][:, :, 0:2], early_rows[:, :, cols])
         for j in (2, 3):
-            gather(late_rows[:, j - 2, :], 1, j, halves[0])
-            gather(last_picked[1][:, :, j], 1, j, halves[1])
-        weave_x(nc.scalar.copy, last_picked[0][:, :, 2:4], late_rows[:])
-        for h in (1, 0):
-            quantise_x(1, halves[h], last_picked[h][:])
+            for h, cols in enumerate(halves):
+                gather(late_rows[h][:, j - 2, :], 1, j, cols)
+        for h, share in enumerate(LATE_VECTOR):
+            weave_x(nc.scalar.copy, last_picked[h][:, share:, 2:4], late_rows[h][:, :, share:])
+            weave_x(nc.vector.tensor_copy, last_picked[h][:, :share, 2:4], late_rows[h][:, :, :share])
+        for h, cols in enumerate(halves):
+            quantise_x(1, cols, last_picked[h][:])
 
         spans = {t: [slice(0, S)] if t == SCALAR_PLANE else [slice(0, HALF), slice(HALF, S)] for t in range(PACK)}
         hidden = {}
@@ -174,14 +176,15 @@ def tile_picked_inorm_none_e_kernel(tc, xT, w1, w2_words, w2_scales, gamma, offs
         for first in (True, False):
             nc.tensor.matmul_mx(
                 out=unread[:],
-                lhsT=x_codes[1][:, S - P :].bitcast(FP8X4),
-                lhsT_scale=x_scales[1][:, S - P :],
+                lhsT=x_codes[1][:, :P].bitcast(FP8X4),
+                lhsT_scale=x_scales[1][:, :P],
                 rhs=x_codes[0][:].bitcast(FP8X4),
                 rhs_scale=x_scales[0][:],
                 start=first,
                 stop=not first,
             )
-        deal(*W_PIECES[0])
+        for t in range(0, PACK, 2):
+            deal(*W_PIECES[0], planes=slice(t, t + 2))
         for t in range(0, PACK, 2):
             quantise_w(0, t, t + 2)
             project(0, t, first=True)

@@ -23,7 +23,7 @@ PASSES = K // (P * PACK)
 HALF = S // 2
 CHUNK = 128
 M_HALF = P // 2
-W_PIECES = ((0, 0, P, 76), (1, 0, M_HALF, 16), (1, M_HALF, P, 42))
+W_PIECES = ((0, 0, P, 76), (1, 0, M_HALF, 26), (1, M_HALF, P, 42))
 SCALAR_PLANE = 1
 LATE_VECTOR = (84, 152)
 
@@ -79,8 +79,6 @@ def tile_picked_inorm_none_e_kernel(tc, xT, w1, w2_words, w2_scales, gamma, offs
         warm_out = sbuf("warm_out", [P, 1], F32)
         nc.vector.memset(warm_in[:], 1.0)
         nc.scalar.activation(warm_out[:], warm_in[:], ACT.Abs_reciprocal_sqrt, bias=EPS)
-        neg_gain = sbuf("neg_gain", [P, PACK], F32)
-        nc.gpsimd.tensor_scalar(neg_gain[:], gain[:], -1.0, 0.0, ALU.mult, ALU.add)
         moments = []
         for t in range(PACK):
             moments.append(sbuf("moments%d" % t, [P, 4], F32))
@@ -196,6 +194,8 @@ def tile_picked_inorm_none_e_kernel(tc, xT, w1, w2_words, w2_scales, gamma, offs
             quantise_w(1, t, t + 1)
             project(1, t, first=False)
 
+        neg_gain = sbuf("neg_gain", [P, PACK], F32, tag="w_codes1")
+        nc.gpsimd.tensor_scalar(neg_gain[:], gain[:], -1.0, 0.0, ALU.mult, ALU.add)
         z_planes = sbuf("z_planes", [P, PACK, S], BF16)
         affine = {}
         inv_std = {}

@@ -295,7 +295,7 @@ def tile_picked_inorm_none_e_kernel(tc, xT, w1, w2_words, w2_scales, gamma, offs
                 acc = psum.tile([P, CHUNK], F32, name="acc%d%d" % (c, m), tag=banks[2 * c + m])
                 second_product(acc[:], m, *codes[c])
                 copy(out=result[:, m, :], in_=acc[:])
-            for rows in [slice(0, 2)] if c < chunks - 1 else [slice(0, 1), slice(1, 2)]:
+            for rows in [slice(0, 2)] if c > 0 else [slice(0, 1), slice(1, 2)]:
                 nc.sync.dma_start(out=out_rows[:, rows, c * CHUNK : (c + 1) * CHUNK], in_=result[:, rows, :])
 
         weave(nc.vector.tensor_copy, 0, 0, CHUNK)

@@ -22,10 +22,16 @@ PACK = 4
 PASSES = K // (P * PACK)
 HALF = S // 2
 CHUNK = 128
+CHUNKS = S // CHUNK
 M_HALF = P // 2
-W_PIECES = ((0, 0, P, 76), (1, 0, M_HALF, 26), (1, M_HALF, P, 42))
+BN_STATS = 6
+
+DEAL_VECTOR_PASS0 = 76
+DEAL_VECTOR_FIRST_HALF = 26
+DEAL_VECTOR_SECOND_HALF = 42
+LATE_WEAVE_VECTOR = (84, 152)
 SCALAR_PLANE = 1
-LATE_VECTOR = (84, 152)
+LAST_PLANE = PACK - 1
 
 
 def tile_picked_inorm_none_e_kernel(tc, xT, w1, w2_words, w2_scales, gamma, offs, out):
@@ -42,14 +48,14 @@ def tile_picked_inorm_none_e_kernel(tc, xT, w1, w2_words, w2_scales, gamma, offs
         x_rows = xT.rearrange("(g p j) t -> g p j t", p=P, j=PACK)
         w_rows = w1.rearrange("(g p j) c -> g p j c", p=P, j=PACK)
 
-        x_planes = {}
+        x_window = {}
         w_raw = {}
 
         def load_x(g, j0, rows):
             loaded = sbuf("x_rows%d%d" % (g, j0), [P, rows, T], F32)
             nc.sync.dma_start(out=loaded[:], in_=x_rows[g][:, j0 : j0 + rows])
             for j in range(rows):
-                x_planes[g, j0 + j] = loaded[:, j, :]
+                x_window[g, j0 + j] = loaded[:, j, :]
 
         def load_w(g, m0, m1):
             w_raw[g, m0] = sbuf("w_rows%d%d" % (g, m0), [P, PACK, PACK * (m1 - m0)], F32)
@@ -67,11 +73,11 @@ def tile_picked_inorm_none_e_kernel(tc, xT, w1, w2_words, w2_scales, gamma, offs
         nc.sync.dma_start(out=gain[:], in_=gamma.rearrange("(p t) o -> p (t o)", t=PACK))
         w2_codes = sbuf("w2_codes", [P, 2 * N], U8)
         nc.sync.dma_start(out=w2_codes[:].bitcast(I32), in_=w2_words[0].bitcast(I32))
-        w2_plane = sbuf("w2_plane", [P, N], U8)
-        nc.gpsimd.memset(w2_plane[:], 0)
+        w2_scale_rows = sbuf("w2_scale_rows", [P, N], U8)
+        nc.gpsimd.memset(w2_scale_rows[:], 0)
         for q in range(4):
             nc.sync.dma_start(
-                out=w2_plane[32 * q : 32 * q + 4, :].bitcast(I32),
+                out=w2_scale_rows[32 * q : 32 * q + 4, :].bitcast(I32),
                 in_=w2_scales[0, 4 * q : 4 * q + 4, :].bitcast(I32),
             )
 
@@ -79,85 +85,80 @@ def tile_picked_inorm_none_e_kernel(tc, xT, w1, w2_words, w2_scales, gamma, offs
         warm_out = sbuf("warm_out", [P, 1], F32)
         nc.vector.memset(warm_in[:], 1.0)
         nc.scalar.activation(warm_out[:], warm_in[:], ACT.Abs_reciprocal_sqrt, bias=EPS)
-        moments = []
+
+        constants = {0: (-float(HALF), -1.0), SCALAR_PLANE: (-float(S),), 2: (-1.0,), LAST_PLANE: (-1.0,)}
+        moments, mean_at = {}, {}
         for t in range(PACK):
-            moments.append(sbuf("moments%d" % t, [P, 4], F32))
-            nc.vector.memset(moments[t][:, 0:1], -float(S if t == SCALAR_PLANE else HALF))
-            nc.vector.memset(moments[t][:, 1:2], -1.0)
+            mean_at[t] = len(constants[t])
+            moments[t] = sbuf("moments%d" % t, [P, mean_at[t] + 2], F32)
+            for at, value in enumerate(constants[t]):
+                nc.vector.memset(moments[t][:, at : at + 1], value)
 
         halves = [slice(0, HALF), slice(HALF, S)]
+        all_points = slice(0, S)
         x_codes = [sbuf("x_codes%d" % g, [P, S], U32) for g in range(PASSES)]
         x_scales = [sbuf("x_scales%d" % g, [P, S], U8) for g in range(PASSES)]
 
-        def gather(target, g, j, cols):
-            entries = offsets[:, cols.start // 16 : cols.stop // 16]
-            nc.vector.tensor_copy(target, x_planes[g, j].indirect(entries))
+        def gather(target, g, j, points):
+            entries = offsets[:, points.start // 16 : points.stop // 16]
+            nc.vector.tensor_copy(target, x_window[g, j].indirect(entries))
 
-        def weave_x(copy, target, source):
+        def weave(copy, target, source):
             copy(
                 out=target.rearrange("p (c i) j -> p c j i", i=4),
                 in_=source.rearrange("p j (c i) -> p c j i", i=4),
             )
 
-        def quantise_x(g, cols, source):
+        def quantise_x(g, points, source):
             nc.vector.quantize_mx(
-                out=x_codes[g][:, cols].bitcast(FP8X4),
-                scales=x_scales[g][:, cols],
+                out=x_codes[g][:, points].bitcast(FP8X4),
+                scales=x_scales[g][:, points],
                 in_=source.rearrange("p s j -> p (s j)"),
             )
 
-        everything = slice(0, S)
         first_rows = sbuf("first_rows", [P, PACK, S], F32)
         first_picked = sbuf("first_picked", [P, S, PACK], BF16)
         for j in range(PACK):
-            gather(first_rows[:, j, :], 0, j, everything)
-        weave_x(nc.vector.tensor_copy, first_picked[:, :HALF], first_rows[:, :, :HALF])
-        weave_x(nc.scalar.copy, first_picked[:, HALF:], first_rows[:, :, HALF:])
+            gather(first_rows[:, j, :], 0, j, all_points)
+        weave(nc.vector.tensor_copy, first_picked[:, :HALF], first_rows[:, :, :HALF])
+        weave(nc.scalar.copy, first_picked[:, HALF:], first_rows[:, :, HALF:])
         early_rows = sbuf("early_rows", [P, 2, S], F32)
         for j in range(2):
-            gather(early_rows[:, j, :], 1, j, everything)
-        quantise_x(0, everything, first_picked[:])
+            gather(early_rows[:, j, :], 1, j, all_points)
+        quantise_x(0, all_points, first_picked[:])
         last_picked = [sbuf("last_picked%d" % h, [P, HALF, PACK], BF16) for h in range(2)]
         late_rows = [sbuf("late_rows%d" % h, [P, 2, HALF], F32) for h in range(2)]
-        for h, cols in enumerate(halves):
-            weave_x(nc.scalar.copy, last_picked[h][:, :, 0:2], early_rows[:, :, cols])
+        for h, points in enumerate(halves):
+            weave(nc.scalar.copy, last_picked[h][:, :, 0:2], early_rows[:, :, points])
         for j in (2, 3):
-            for h, cols in enumerate(halves):
-                gather(late_rows[h][:, j - 2, :], 1, j, cols)
-        for h, share in enumerate(LATE_VECTOR):
-            weave_x(nc.scalar.copy, last_picked[h][:, share:, 2:4], late_rows[h][:, :, share:])
-            weave_x(nc.vector.tensor_copy, last_picked[h][:, :share, 2:4], late_rows[h][:, :, :share])
-        for h, cols in enumerate(halves):
-            quantise_x(1, cols, last_picked[h][:])
+            for h, points in enumerate(halves):
+                gather(late_rows[h][:, j - 2, :], 1, j, points)
+        for h, share in enumerate(LATE_WEAVE_VECTOR):
+            weave(nc.scalar.copy, last_picked[h][:, share:, 2:4], late_rows[h][:, :, share:])
+            weave(nc.vector.tensor_copy, last_picked[h][:, :share, 2:4], late_rows[h][:, :, :share])
+        for h, points in enumerate(halves):
+            quantise_x(1, points, last_picked[h][:])
 
-        spans = {t: [slice(0, S)] if t == SCALAR_PLANE else [slice(0, HALF), slice(HALF, S)] for t in range(PACK)}
+        spans = {t: [all_points] if t == SCALAR_PLANE else halves for t in range(PACK)}
         hidden = {}
         for t in range(PACK):
-            for piece, cols in enumerate(spans[t]):
+            for piece, points in enumerate(spans[t]):
                 hidden[t, piece] = psum.tile(
-                    [P, cols.stop - cols.start], F32, name="hidden%d%d" % (t, piece), tag="bank%d%d" % (t, piece)
+                    [P, points.stop - points.start], F32, name="hidden%d%d" % (t, piece), tag="bank%d%d" % (t, piece)
                 )
 
-        partial = {t: sbuf("partial%d" % t, [P, 9 if t == 0 else 12], F32) for t in range(PACK) if t != SCALAR_PLANE}
-        nc.vector.memset(partial[0][:, 6:7], float(HALF))
-
-        def project(g, t, first):
-            for piece, cols in enumerate(spans[t]):
-                nc.tensor.matmul_mx(
-                    out=hidden[t, piece][:],
-                    lhsT=w_codes[g][:, P * t : P * (t + 1)].bitcast(FP8X4),
-                    lhsT_scale=w_scales[g][:, P * t : P * (t + 1)],
-                    rhs=x_codes[g][:, cols].bitcast(FP8X4),
-                    rhs_scale=x_scales[g][:, cols],
-                    start=first,
-                    stop=not first,
-                )
+        triples = {
+            0: sbuf("triples0", [P, BN_STATS + 3], F32),
+            2: sbuf("triples2", [P, 2 * BN_STATS], F32),
+            LAST_PLANE: sbuf("triples3", [P, 2 * BN_STATS], F32),
+        }
+        nc.vector.memset(triples[0][:, BN_STATS : BN_STATS + 1], float(HALF))
 
         w_codes = [sbuf("w_codes%d" % g, [P, H], U32) for g in range(PASSES)]
         w_scales = [sbuf("w_scales%d" % g, [P, H], U8) for g in range(PASSES)]
         dealt = [sbuf("dealt%d" % g, [P, PACK, P, PACK], BF16) for g in range(PASSES)]
 
-        def deal(g, m0, m1, vector_share, planes=slice(0, PACK)):
+        def deal(g, m0, m1, vector_share, planes):
             source = w_raw[g, m0][:].rearrange("p j (m t) -> p m j t", t=PACK)[:, :, :, planes]
             target = dealt[g][:, planes, m0:m1, :].rearrange("p t m j -> p m j t")
             nc.vector.tensor_copy(out=target[:, :vector_share], in_=source[:, :vector_share])
@@ -170,6 +171,18 @@ def tile_picked_inorm_none_e_kernel(tc, xT, w1, w2_words, w2_scales, gamma, offs
                 in_=dealt[g][:, t0:t1].rearrange("p t m j -> p (t m j)"),
             )
 
+        def first_product(g, t):
+            for piece, points in enumerate(spans[t]):
+                nc.tensor.matmul_mx(
+                    out=hidden[t, piece][:],
+                    lhsT=w_codes[g][:, P * t : P * (t + 1)].bitcast(FP8X4),
+                    lhsT_scale=w_scales[g][:, P * t : P * (t + 1)],
+                    rhs=x_codes[g][:, points].bitcast(FP8X4),
+                    rhs_scale=x_scales[g][:, points],
+                    start=(g == 0),
+                    stop=(g == PASSES - 1),
+                )
+
         unread = psum.tile([P, S], F32, name="unread", tag="spare")
         for first in (True, False):
             nc.tensor.matmul_mx(
@@ -181,131 +194,130 @@ def tile_picked_inorm_none_e_kernel(tc, xT, w1, w2_words, w2_scales, gamma, offs
                 start=first,
                 stop=not first,
             )
-        for t in range(0, PACK, 2):
-            deal(*W_PIECES[0], planes=slice(t, t + 2))
-        for t in range(0, PACK, 2):
-            quantise_w(0, t, t + 2)
-            project(0, t, first=True)
-            project(0, t + 1, first=True)
-        deal(*W_PIECES[1])
-        deal(*W_PIECES[2], planes=slice(0, 2))
-        deal(*W_PIECES[2], planes=slice(2, PACK))
+
+        pairs = [slice(0, 2), slice(2, PACK)]
+        for planes in pairs:
+            deal(0, 0, P, DEAL_VECTOR_PASS0, planes)
+        for planes in pairs:
+            quantise_w(0, planes.start, planes.stop)
+            for t in range(planes.start, planes.stop):
+                first_product(0, t)
+        deal(1, 0, M_HALF, DEAL_VECTOR_FIRST_HALF, slice(0, PACK))
+        for planes in pairs:
+            deal(1, M_HALF, P, DEAL_VECTOR_SECOND_HALF, planes)
         for t in range(PACK):
             quantise_w(1, t, t + 1)
-            project(1, t, first=False)
+            first_product(1, t)
 
         neg_gain = sbuf("neg_gain", [P, PACK], F32, tag="w_codes1")
         nc.gpsimd.tensor_scalar(neg_gain[:], gain[:], -1.0, 0.0, ALU.mult, ALU.add)
         z_planes = sbuf("z_planes", [P, PACK, S], BF16)
-        affine = {}
-        inv_std = {}
 
-        def coefficients(t):
-            affine[t] = sbuf("affine%d" % t, [P, 3], F32)
-            nc.vector.tensor_scalar(
-                affine[t][:], moments[t][:, 0:3], inv_std[t][:], neg_gain[:, t : t + 1], ALU.mult, ALU.mult
-            )
-
-        evacuated = {(0, 0): sbuf("evacuated0", [P, HALF], F32), (1, 0): sbuf("evacuated1", [P, S], F32)}
-        squares = sbuf("squares", [P, S + HALF], F32)
-        mean_at = {(0, 0): partial[0][:, 7:8], (1, 0): moments[1][:, 2:3]}
-        spread_at = {(0, 0): partial[0][:, 8:9], (1, 0): moments[1][:, 3:4]}
-        for key, copy in evacuated.items():
-            nc.scalar.activation(copy[:], hidden[key][:], ACT.Identity, scale=1.0 / copy.shape[1], accum_out=mean_at[key])
-        for key, copy in evacuated.items():
+        scaled_copy = {(0, 0): sbuf("scaled_copy0", [P, HALF], F32), (SCALAR_PLANE, 0): sbuf("scaled_copy1", [P, S], F32)}
+        squares = sbuf("squares", [P, HALF + S], F32)
+        scalar_moments = {
+            (0, 0): triples[0][:, BN_STATS + 1 :],
+            (SCALAR_PLANE, 0): moments[SCALAR_PLANE][:, mean_at[SCALAR_PLANE] :],
+        }
+        squares_part = {(0, 0): squares[:, :HALF], (SCALAR_PLANE, 0): squares[:, HALF:]}
+        for key, target in scaled_copy.items():
             nc.scalar.activation(
-                squares[:, HALF * key[0] : HALF * key[0] + copy.shape[1]],
+                target[:], hidden[key][:], ACT.Identity, scale=1.0 / target.shape[1], accum_out=scalar_moments[key][:, 0:1]
+            )
+        for key in scaled_copy:
+            nc.scalar.activation(
+                squares_part[key],
                 hidden[key][:],
                 ACT.Square,
-                bias=mean_at[key],
+                bias=scalar_moments[key][:, 0:1],
                 scale=-1.0,
-                accum_out=spread_at[key],
+                accum_out=scalar_moments[key][:, 1:2],
             )
+        affine = {}
         for t in range(PACK):
-            inv_std[t] = sbuf("inv_std%d" % t, [P, 1], F32)
-            for half in range(len(spans[t])):
-                if (t, half) not in evacuated:
-                    at = 0 if t == 0 else 6 * half
-                    nc.vector.bn_stats(partial[t][:, at : at + 6], hidden[t, half][:])
+            inv_std = sbuf("inv_std%d" % t, [P, 1], F32)
+            spread = moments[t][:, mean_at[t] + 1 :]
             if t == SCALAR_PLANE:
-                nc.scalar.activation(inv_std[t][:], moments[t][:, 3:4], ACT.Abs_reciprocal_sqrt, bias=EPS, scale=1.0 / S)
+                nc.scalar.activation(inv_std[:], spread, ACT.Abs_reciprocal_sqrt, bias=EPS, scale=1.0 / S)
             else:
-                nc.vector.bn_aggr(moments[t][:, 2:4], partial[t][:])
-                nc.scalar.activation(inv_std[t][:], moments[t][:, 3:4], ACT.Abs_reciprocal_sqrt, bias=EPS)
-            coefficients(t)
-
-        def normalise_vector(t, source, cols, factor):
+                by_vector = [half for half in range(2) if (t, half) not in scaled_copy]
+                for n, half in enumerate(by_vector):
+                    nc.vector.bn_stats(triples[t][:, BN_STATS * n : BN_STATS * (n + 1)], hidden[t, half][:])
+                nc.vector.bn_aggr(moments[t][:, mean_at[t] :], triples[t][:])
+                nc.scalar.activation(inv_std[:], spread, ACT.Abs_reciprocal_sqrt, bias=EPS)
+            affine[t] = sbuf("affine%d" % t, [P, mean_at[t] + 1], F32)
             nc.vector.tensor_scalar(
-                z_planes[:, t, cols], source, affine[t][:, factor : factor + 1], affine[t][:, 2:3], ALU.mult, ALU.add
+                affine[t][:], moments[t][:, : mean_at[t] + 1], inv_std[:], neg_gain[:, t : t + 1], ALU.mult, ALU.mult
             )
+
+        def shift(t):
+            return affine[t][:, mean_at[t] :]
+
+        def copy_factor(t):
+            return affine[t][:, 0:1]
+
+        def psum_factor(t):
+            return affine[t][:, mean_at[t] - 1 : mean_at[t]]
+
+        def normalise_vector(t, source, points, factor):
+            nc.vector.tensor_scalar(z_planes[:, t, points], source, factor, shift(t), ALU.mult, ALU.add)
 
         for t, half in hidden:
-            cols = spans[t][half]
-            if (t, half) in evacuated:
-                normalise_vector(t, evacuated[t, half][:, :HALF], halves[0], 0)
-            elif (t, half) == (2, 0):
-                normalise_vector(t, hidden[t, half][:], cols, 1)
-            elif (t, half) == (3, 0):
-                for c in range(2):
-                    part = slice(c * CHUNK, (c + 1) * CHUNK)
-                    normalise_vector(t, hidden[t, half][:, part], part, 1)
+            if (t, half) in scaled_copy:
+                normalise_vector(t, scaled_copy[t, half][:, :HALF], halves[0], copy_factor(t))
+            elif half == 0:
+                width = CHUNK if t == LAST_PLANE else HALF
+                for s0 in range(0, HALF, width):
+                    points = slice(s0, s0 + width)
+                    normalise_vector(t, hidden[t, half][:, points], points, psum_factor(t))
             else:
                 nc.scalar.activation(
-                    z_planes[:, t, cols], hidden[t, half][:], ACT.Identity, bias=affine[t][:, 2:3], scale=affine[t][:, 1:2]
+                    z_planes[:, t, halves[1]], hidden[t, half][:], ACT.Identity, bias=shift(t), scale=psum_factor(t)
                 )
+        normalise_vector(SCALAR_PLANE, scaled_copy[SCALAR_PLANE, 0][:, HALF:], halves[1], copy_factor(SCALAR_PLANE))
 
-        normalise_vector(SCALAR_PLANE, evacuated[SCALAR_PLANE, 0][:, HALF:], halves[1], 0)
-
-        chunks = S // CHUNK
-        woven = [sbuf("woven%d" % c, [P, CHUNK, PACK], BF16) for c in range(chunks)]
-
-        def weave(copy, c, s0, s1):
-            copy(
-                out=woven[c][:, s0:s1, :].rearrange("p (c i) t -> p c t i", i=4),
-                in_=z_planes[:, :, c * CHUNK + s0 : c * CHUNK + s1].rearrange("p t (c i) -> p c t i", i=4),
-            )
-
+        woven = [sbuf("woven%d" % c, [P, CHUNK, PACK], BF16) for c in range(CHUNKS)]
+        z_codes = [sbuf("z_codes%d" % c, [P, CHUNK], U32) for c in range(CHUNKS)]
+        z_scales = [sbuf("z_scales%d" % c, [P, CHUNK], U8) for c in range(CHUNKS)]
         out_rows = out.rearrange("(m p) s -> p m s", p=P)
         banks = ["spare"] + ["bank%d%d" % key for key in hidden]
 
-        def second_product(acc, m, z_codes, z_scales):
-            nc.tensor.matmul_mx(
-                out=acc,
-                lhsT=w2_codes[:, 2 * P * m : 2 * P * (m + 1)].bitcast(FP4X4),
-                lhsT_scale=w2_plane[:, P * m : P * (m + 1)],
-                rhs=z_codes[:].bitcast(FP8X4),
-                rhs_scale=z_scales[:],
-                start=True,
-                stop=True,
-            )
+        def weave_z(copy, c, s0, s1):
+            weave(copy, woven[c][:, s0:s1, :], z_planes[:, :, c * CHUNK + s0 : c * CHUNK + s1])
 
         def quantise_z(c):
-            z_codes = sbuf("z_codes%d" % c, [P, CHUNK], U32)
-            z_scales = sbuf("z_scales%d" % c, [P, CHUNK], U8)
             nc.vector.quantize_mx(
-                out=z_codes[:].bitcast(FP8X4),
-                scales=z_scales[:],
+                out=z_codes[c][:].bitcast(FP8X4),
+                scales=z_scales[c][:],
                 in_=woven[c][:].rearrange("p s t -> p (s t)"),
             )
-            return z_codes, z_scales
 
-        def second_layer(c, copies):
+        def second_product(c, copies, stores):
             result = sbuf("result%d" % c, [P, N // P, CHUNK], F32)
             for m, copy in enumerate(copies):
                 acc = psum.tile([P, CHUNK], F32, name="acc%d%d" % (c, m), tag=banks[2 * c + m])
-                second_product(acc[:], m, *codes[c])
+                nc.tensor.matmul_mx(
+                    out=acc[:],
+                    lhsT=w2_codes[:, 2 * P * m : 2 * P * (m + 1)].bitcast(FP4X4),
+                    lhsT_scale=w2_scale_rows[:, P * m : P * (m + 1)],
+                    rhs=z_codes[c][:].bitcast(FP8X4),
+                    rhs_scale=z_scales[c][:],
+                    start=True,
+                    stop=True,
+                )
                 copy(out=result[:, m, :], in_=acc[:])
-            for rows in [slice(0, 2)] if c > 0 else [slice(0, 1), slice(1, 2)]:
-                nc.sync.dma_start(out=out_rows[:, rows, c * CHUNK : (c + 1) * CHUNK], in_=result[:, rows, :])
+            for blocks in stores:
+                nc.sync.dma_start(out=out_rows[:, blocks, c * CHUNK : (c + 1) * CHUNK], in_=result[:, blocks, :])
 
-        weave(nc.vector.tensor_copy, 0, 0, CHUNK)
-        weave(nc.scalar.copy, 2, 0, CHUNK)
-        weave(nc.scalar.copy, 3, 0, CHUNK // 2)
-        codes = [quantise_z(0)]
-        weave(nc.vector.tensor_copy, 1, 0, CHUNK)
-        codes.append(quantise_z(1))
-        weave(nc.vector.tensor_copy, 3, CHUNK // 2, CHUNK)
-        codes.extend(quantise_z(c) for c in (2, 3))
-        second_layer(0, [nc.scalar.copy, nc.scalar.copy])
-        for c in range(1, chunks):
-            second_layer(c, [nc.scalar.copy, nc.vector.tensor_copy])
+        weave_z(nc.vector.tensor_copy, 0, 0, CHUNK)
+        weave_z(nc.scalar.copy, 2, 0, CHUNK)
+        weave_z(nc.scalar.copy, 3, 0, CHUNK // 2)
+        quantise_z(0)
+        weave_z(nc.vector.tensor_copy, 1, 0, CHUNK)
+        quantise_z(1)
+        weave_z(nc.vector.tensor_copy, 3, CHUNK // 2, CHUNK)
+        quantise_z(2)
+        quantise_z(3)
+        second_product(0, [nc.scalar.copy, nc.scalar.copy], [slice(0, 1), slice(1, 2)])
+        for c in range(1, CHUNKS):
+            second_product(c, [nc.scalar.copy, nc.vector.tensor_copy], [slice(0, 2)])

@@ -154,7 +154,7 @@ def tile_picked_inorm_none_e_kernel(tc, xT, w1, w2_words, w2_scales, gamma, offs
         }
         nc.vector.memset(triples[0][:, BN_STATS : BN_STATS + 1], float(HALF))
 
-        w_codes = [sbuf("w_codes%d" % g, [P, H], U32) for g in range(PASSES)]
+        w_codes = [sbuf("w_codes0", [P, LAST_PLANE * P], U32), sbuf("w_codes1", [P, H], U32)]
         w_scales = [sbuf("w_scales%d" % g, [P, H], U8) for g in range(PASSES)]
         dealt = [sbuf("dealt%d" % g, [P, PACK, P, PACK], BF16) for g in range(PASSES)]
 
@@ -164,24 +164,30 @@ def tile_picked_inorm_none_e_kernel(tc, xT, w1, w2_words, w2_scales, gamma, offs
             nc.vector.tensor_copy(out=target[:, :vector_share], in_=source[:, :vector_share])
             nc.scalar.copy(out=target[:, vector_share:], in_=source[:, vector_share:])
 
-        def quantise_w(g, t0, t1):
+        stationary = {}
+
+        def quantise_w(g, t0, t1, codes):
             nc.vector.quantize_mx(
-                out=w_codes[g][:, P * t0 : P * t1].bitcast(FP8X4),
+                out=codes.bitcast(FP8X4),
                 scales=w_scales[g][:, P * t0 : P * t1],
                 in_=dealt[g][:, t0:t1].rearrange("p t m j -> p (t m j)"),
             )
+            for t in range(t0, t1):
+                stationary[g, t] = codes[:, P * (t - t0) : P * (t - t0 + 1)]
 
-        def first_product(g, t):
-            for piece, points in enumerate(spans[t]):
-                nc.tensor.matmul_mx(
-                    out=hidden[t, piece][:],
-                    lhsT=w_codes[g][:, P * t : P * (t + 1)].bitcast(FP8X4),
-                    lhsT_scale=w_scales[g][:, P * t : P * (t + 1)],
-                    rhs=x_codes[g][:, points].bitcast(FP8X4),
-                    rhs_scale=x_scales[g][:, points],
-                    start=(g == 0),
-                    stop=(g == PASSES - 1),
-                )
+        pass_order = {t: (1, 0) if t == LAST_PLANE else (0, 1) for t in range(PACK)}
+
+        def first_product(g, t, piece):
+            points = spans[t][piece]
+            nc.tensor.matmul_mx(
+                out=hidden[t, piece][:],
+                lhsT=stationary[g, t].bitcast(FP8X4),
+                lhsT_scale=w_scales[g][:, P * t : P * (t + 1)],
+                rhs=x_codes[g][:, points].bitcast(FP8X4),
+                rhs_scale=x_scales[g][:, points],
+                start=(g == pass_order[t][0]),
+                stop=(g == pass_order[t][-1]),
+            )
 
         unread = psum.tile([P, S], F32, name="unread", tag="spare")
         for first in (True, False):
@@ -198,16 +204,22 @@ def tile_picked_inorm_none_e_kernel(tc, xT, w1, w2_words, w2_scales, gamma, offs
         pairs = [slice(0, 2), slice(2, PACK)]
         for planes in pairs:
             deal(0, 0, P, DEAL_VECTOR_PASS0, planes)
-        for planes in pairs:
-            quantise_w(0, planes.start, planes.stop)
-            for t in range(planes.start, planes.stop):
-                first_product(0, t)
+        for t0, t1 in ((0, 2), (2, LAST_PLANE)):
+            quantise_w(0, t0, t1, w_codes[0][:, P * t0 : P * t1])
+            for t in range(t0, t1):
+                for piece in range(len(spans[t])):
+                    first_product(0, t, piece)
         deal(1, 0, M_HALF, DEAL_VECTOR_FIRST_HALF, slice(0, PACK))
         for planes in pairs:
             deal(1, M_HALF, P, DEAL_VECTOR_SECOND_HALF, planes)
         for t in range(PACK):
-            quantise_w(1, t, t + 1)
-            first_product(1, t)
+            quantise_w(1, t, t + 1, w_codes[1][:, P * t : P * (t + 1)])
+        late_codes = sbuf("late_codes", [P, P], U32, tag="w_rows1%d" % M_HALF)
+        quantise_w(0, LAST_PLANE, PACK, late_codes[:])
+        for t in range(PACK):
+            for piece in range(len(spans[t])):
+                for g in pass_order[t][t != LAST_PLANE :]:
+                    first_product(g, t, piece)
 
         neg_gain = sbuf("neg_gain", [P, PACK], F32, tag="w_codes1")
         nc.gpsimd.tensor_scalar(neg_gain[:], gain[:], -1.0, 0.0, ALU.mult, ALU.add)

@@ -103,10 +103,10 @@ def tile_picked_inorm_none_e_kernel(tc, xT, w1, w2_words, w2_scales, gamma, offs
             entries = offsets[:, points.start // 16 : points.stop // 16]
             nc.vector.tensor_copy(target, x_window[g, j].indirect(entries))
 
-        def weave(copy, target, source):
+        def weave(copy, target, source, run=4):
             copy(
-                out=target.rearrange("p (c i) j -> p c j i", i=4),
-                in_=source.rearrange("p j (c i) -> p c j i", i=4),
+                out=target.rearrange("p (c i) j -> p c j i", i=run),
+                in_=source.rearrange("p j (c i) -> p c j i", i=run),
             )
 
         def quantise_x(g, points, source):
@@ -246,20 +246,23 @@ def tile_picked_inorm_none_e_kernel(tc, xT, w1, w2_words, w2_scales, gamma, offs
                 accum_out=scalar_moments[key][:, 1:2],
             )
         affine = {}
-        for t in range(PACK):
-            inv_std = sbuf("inv_std%d" % t, [P, 1], F32)
+        inv_std = {}
+        for t in (0, 2, SCALAR_PLANE, LAST_PLANE):
+            inv_std[t] = sbuf("inv_std%d" % t, [P, 1], F32)
             spread = moments[t][:, mean_at[t] + 1 :]
             if t == SCALAR_PLANE:
-                nc.scalar.activation(inv_std[:], spread, ACT.Abs_reciprocal_sqrt, bias=EPS, scale=1.0 / S)
+                nc.scalar.activation(inv_std[t][:], spread, ACT.Abs_reciprocal_sqrt, bias=EPS, scale=1.0 / S)
             else:
                 by_vector = [half for half in range(2) if (t, half) not in scaled_copy]
                 for n, half in enumerate(by_vector):
                     nc.vector.bn_stats(triples[t][:, BN_STATS * n : BN_STATS * (n + 1)], hidden[t, half][:])
                 nc.vector.bn_aggr(moments[t][:, mean_at[t] :], triples[t][:])
-                nc.scalar.activation(inv_std[:], spread, ACT.Abs_reciprocal_sqrt, bias=EPS)
+                nc.scalar.activation(inv_std[t][:], spread, ACT.Abs_reciprocal_sqrt, bias=EPS)
+
+        def coefficients(t):
             affine[t] = sbuf("affine%d" % t, [P, mean_at[t] + 1], F32)
             nc.vector.tensor_scalar(
-                affine[t][:], moments[t][:, : mean_at[t] + 1], inv_std[:], neg_gain[:, t : t + 1], ALU.mult, ALU.mult
+                affine[t][:], moments[t][:, : mean_at[t] + 1], inv_std[t][:], neg_gain[:, t : t + 1], ALU.mult, ALU.mult
             )
 
         def shift(t):
@@ -274,19 +277,22 @@ def tile_picked_inorm_none_e_kernel(tc, xT, w1, w2_words, w2_scales, gamma, offs
         def normalise_vector(t, source, points, factor):
             nc.vector.tensor_scalar(z_planes[:, t, points], source, factor, shift(t), ALU.mult, ALU.add)
 
-        for t, half in hidden:
-            if (t, half) in scaled_copy:
-                normalise_vector(t, scaled_copy[t, half][:, :HALF], halves[0], copy_factor(t))
-            elif half == 0:
-                width = CHUNK if t == LAST_PLANE else HALF
-                for s0 in range(0, HALF, width):
-                    points = slice(s0, s0 + width)
-                    normalise_vector(t, hidden[t, half][:, points], points, psum_factor(t))
-            else:
-                nc.scalar.activation(
-                    z_planes[:, t, halves[1]], hidden[t, half][:], ACT.Identity, bias=shift(t), scale=psum_factor(t)
-                )
+        def normalise_scalar(t, source, points):
+            nc.scalar.activation(z_planes[:, t, points], source, ACT.Identity, bias=shift(t), scale=psum_factor(t))
+
+        chunks = [slice(c * CHUNK, (c + 1) * CHUNK) for c in range(CHUNKS)]
+        coefficients(0)
+        coefficients(2)
+        normalise_vector(0, scaled_copy[0, 0][:], halves[0], copy_factor(0))
+        coefficients(SCALAR_PLANE)
+        normalise_vector(2, hidden[2, 0][:], halves[0], psum_factor(2))
+        coefficients(LAST_PLANE)
+        normalise_vector(SCALAR_PLANE, scaled_copy[SCALAR_PLANE, 0][:, :HALF], halves[0], copy_factor(SCALAR_PLANE))
+        normalise_vector(LAST_PLANE, hidden[LAST_PLANE, 0][:, chunks[0]], chunks[0], psum_factor(LAST_PLANE))
         normalise_vector(SCALAR_PLANE, scaled_copy[SCALAR_PLANE, 0][:, HALF:], halves[1], copy_factor(SCALAR_PLANE))
+        for t in (0, 2, LAST_PLANE):
+            normalise_scalar(t, hidden[t, 1][:], halves[1])
+        normalise_scalar(LAST_PLANE, hidden[LAST_PLANE, 0][:, chunks[1]], chunks[1])
 
         woven = [sbuf("woven%d" % c, [P, CHUNK, PACK], BF16) for c in range(CHUNKS)]
         z_codes = [sbuf("z_codes%d" % c, [P, CHUNK], U32) for c in range(CHUNKS)]
@@ -295,7 +301,7 @@ def tile_picked_inorm_none_e_kernel(tc, xT, w1, w2_words, w2_scales, gamma, offs
         banks = ["spare"] + ["bank%d%d" % key for key in hidden]
 
         def weave_z(copy, c, s0, s1):
-            weave(copy, woven[c][:, s0:s1, :], z_planes[:, :, c * CHUNK + s0 : c * CHUNK + s1])
+            weave(copy, woven[c][:, s0:s1, :], z_planes[:, :, c * CHUNK + s0 : c * CHUNK + s1], run=8)
 
         def quantise_z(c):
             nc.vector.quantize_mx(
@@ -322,14 +328,14 @@ def tile_picked_inorm_none_e_kernel(tc, xT, w1, w2_words, w2_scales, gamma, offs
                 nc.sync.dma_start(out=out_rows[:, blocks, c * CHUNK : (c + 1) * CHUNK], in_=result[:, blocks, :])
 
         weave_z(nc.vector.tensor_copy, 0, 0, CHUNK)
-        weave_z(nc.scalar.copy, 2, 0, CHUNK)
-        weave_z(nc.scalar.copy, 3, 0, CHUNK // 2)
+        weave_z(nc.scalar.copy, 3, 0, CHUNK)
+        weave_z(nc.vector.tensor_copy, 2, 0, CHUNK)
+        weave_z(nc.scalar.copy, 1, CHUNK // 2, CHUNK)
         quantise_z(0)
-        weave_z(nc.vector.tensor_copy, 1, 0, CHUNK)
-        quantise_z(1)
-        weave_z(nc.vector.tensor_copy, 3, CHUNK // 2, CHUNK)
+        weave_z(nc.vector.tensor_copy, 1, 0, CHUNK // 2)
         quantise_z(2)
         quantise_z(3)
+        quantise_z(1)
         second_product(0, [nc.scalar.copy, nc.scalar.copy], [slice(0, 1), slice(1, 2)])
-        for c in range(1, CHUNKS):
+        for c in (2, 3, 1):
             second_product(c, [nc.scalar.copy, nc.vector.tensor_copy], [slice(0, 2)])

@@ -41,7 +41,7 @@ def tile_picked_inorm_none_e_kernel(tc, xT, w1, w2_words, w2_scales, gamma, offs
         psum = ctx.enter_context(tc.psum_pool(name="psum", bufs=1))
 
         def sbuf(name, shape, dtype, tag=None):
-            return keep.tile(shape, dtype, name=name, tag=tag or name, align_bytes=64)
+            return keep.tile(shape, dtype, name=name, tag=tag or name, align_bytes=256)
 
         offsets = keep.tile([P, S // 16], U16, name="offsets")
         gain = sbuf("gain", [P, PACK], F32)

@@ -24,6 +24,7 @@ HALF = S // 2
 CHUNK = 128
 CHUNKS = S // CHUNK
 M_HALF = P // 2
+PACKET = 4096
 BN_STATS = 6
 
 DEAL_VECTOR_PASS0 = 76
@@ -40,8 +41,8 @@ def tile_picked_inorm_none_e_kernel(tc, xT, w1, w2_words, w2_scales, gamma, offs
         keep = ctx.enter_context(tc.tile_pool(name="keep", bufs=1))
         psum = ctx.enter_context(tc.psum_pool(name="psum", bufs=1))
 
-        def sbuf(name, shape, dtype, tag=None):
-            return keep.tile(shape, dtype, name=name, tag=tag or name, align_bytes=256)
+        def sbuf(name, shape, dtype, tag=None, align=256):
+            return keep.tile(shape, dtype, name=name, tag=tag or name, align_bytes=align)
 
         offsets = keep.tile([P, S // 16], U16, name="offsets")
         gain = sbuf("gain", [P, PACK], F32)
@@ -52,13 +53,13 @@ def tile_picked_inorm_none_e_kernel(tc, xT, w1, w2_words, w2_scales, gamma, offs
         w_raw = {}
 
         def load_x(g, j0, rows):
-            loaded = sbuf("x_rows%d%d" % (g, j0), [P, rows, T], F32)
+            loaded = sbuf("x_rows%d%d" % (g, j0), [P, rows, T], F32, align=PACKET)
             nc.sync.dma_start(out=loaded[:], in_=x_rows[g][:, j0 : j0 + rows])
             for j in range(rows):
                 x_window[g, j0 + j] = loaded[:, j, :]
 
         def load_w(g, m0, m1):
-            w_raw[g, m0] = sbuf("w_rows%d%d" % (g, m0), [P, PACK, PACK * (m1 - m0)], F32)
+            w_raw[g, m0] = sbuf("w_rows%d%d" % (g, m0), [P, PACK, PACK * (m1 - m0)], F32, align=PACKET)
             nc.sync.dma_start(out=w_raw[g, m0][:], in_=w_rows[g][:, :, PACK * m0 : PACK * m1])
 
         load_x(0, 0, 2)
@@ -214,7 +215,7 @@ def tile_picked_inorm_none_e_kernel(tc, xT, w1, w2_words, w2_scales, gamma, offs
             deal(1, M_HALF, P, DEAL_VECTOR_SECOND_HALF, planes)
         for t in range(PACK):
             quantise_w(1, t, t + 1, w_codes[1][:, P * t : P * (t + 1)])
-        late_codes = sbuf("late_codes", [P, P], U32, tag="w_rows1%d" % M_HALF)
+        late_codes = sbuf("late_codes", [P, P], U32, tag="w_rows1%d" % M_HALF, align=PACKET)
         quantise_w(0, LAST_PLANE, PACK, late_codes[:])
         for t in range(PACK):
             for piece in range(len(spans[t])):

@@ -76,10 +76,11 @@ def tile_picked_inorm_none_e_kernel(tc, xT, w1, w2_words, w2_scales, gamma, offs
         nc.sync.dma_start(out=w2_codes[:].bitcast(I32), in_=w2_words[0].bitcast(I32))
         w2_scale_rows = sbuf("w2_scale_rows", [P, N], U8)
         nc.gpsimd.memset(w2_scale_rows[:], 0)
-        for q in range(4):
+        for row in range(0, 16, 2):
+            place = 32 * (row // 4) + row % 4
             nc.sync.dma_start(
-                out=w2_scale_rows[32 * q : 32 * q + 4, :].bitcast(I32),
-                in_=w2_scales[0, 4 * q : 4 * q + 4, :].bitcast(I32),
+                out=w2_scale_rows[place : place + 2, :].bitcast(I32),
+                in_=w2_scales[0, row : row + 2, :].bitcast(I32),
             )
 
         warm_in = sbuf("warm_in", [P, 1], F32)

@@ -27,10 +27,10 @@ M_HALF = P // 2
 PACKET = 4096
 BN_STATS = 6
 
-DEAL_VECTOR_PASS0 = 76
-DEAL_VECTOR_FIRST_HALF = 26
+DEAL_VECTOR_PASS0 = 84
+DEAL_VECTOR_FIRST_HALF = 20
 DEAL_VECTOR_SECOND_HALF = 42
-LATE_WEAVE_VECTOR = (84, 152)
+LATE_WEAVE_VECTOR = 96
 SCALAR_PLANE = 1
 LAST_PLANE = PACK - 1
 
@@ -67,8 +67,8 @@ def tile_picked_inorm_none_e_kernel(tc, xT, w1, w2_words, w2_scales, gamma, offs
         load_x(0, 2, 2)
         load_x(1, 0, 2)
         load_x(1, 2, 1)
-        load_x(1, 3, 1)
         load_w(0, 0, P)
+        load_x(1, 3, 1)
         load_w(1, 0, M_HALF)
         load_w(1, M_HALF, P)
         nc.sync.dma_start(out=gain[:], in_=gamma.rearrange("(p t) o -> p (t o)", t=PACK))
@@ -132,14 +132,8 @@ def tile_picked_inorm_none_e_kernel(tc, xT, w1, w2_words, w2_scales, gamma, offs
         late_rows = [sbuf("late_rows%d" % h, [P, 2, HALF], F32) for h in range(2)]
         for h, points in enumerate(halves):
             weave(nc.scalar.copy, last_picked[h][:, :, 0:2], early_rows[:, :, points])
-        for j in (2, 3):
-            for h, points in enumerate(halves):
-                gather(late_rows[h][:, j - 2, :], 1, j, points)
-        for h, share in enumerate(LATE_WEAVE_VECTOR):
-            weave(nc.scalar.copy, last_picked[h][:, share:, 2:4], late_rows[h][:, :, share:])
-            weave(nc.vector.tensor_copy, last_picked[h][:, :share, 2:4], late_rows[h][:, :, :share])
         for h, points in enumerate(halves):
-            quantise_x(1, points, last_picked[h][:])
+            gather(late_rows[h][:, 0, :], 1, 2, points)
 
         spans = {t: [all_points] if t == SCALAR_PLANE else halves for t in range(PACK)}
         hidden = {}
@@ -156,7 +150,7 @@ def tile_picked_inorm_none_e_kernel(tc, xT, w1, w2_words, w2_scales, gamma, offs
         }
         nc.vector.memset(triples[0][:, BN_STATS : BN_STATS + 1], float(HALF))
 
-        w_codes = [sbuf("w_codes0", [P, LAST_PLANE * P], U32), sbuf("w_codes1", [P, H], U32)]
+        w_codes = [sbuf("w_codes0", [P, H], U32), sbuf("w_codes1", [P, H], U32)]
         w_scales = [sbuf("w_scales%d" % g, [P, H], U8) for g in range(PASSES)]
         dealt = [sbuf("dealt%d" % g, [P, PACK, P, PACK], BF16) for g in range(PASSES)]
 
@@ -177,7 +171,7 @@ def tile_picked_inorm_none_e_kernel(tc, xT, w1, w2_words, w2_scales, gamma, offs
             for t in range(t0, t1):
                 stationary[g, t] = codes[:, P * (t - t0) : P * (t - t0 + 1)]
 
-        pass_order = {t: (1, 0) if t == LAST_PLANE else (0, 1) for t in range(PACK)}
+        pass_order = {t: (0, 1) for t in range(PACK)}
 
         def first_product(g, t, piece):
             points = spans[t][piece]
@@ -191,37 +185,47 @@ def tile_picked_inorm_none_e_kernel(tc, xT, w1, w2_words, w2_scales, gamma, offs
                 stop=(g == pass_order[t][-1]),
             )
 
-        unread = psum.tile([P, S], F32, name="unread", tag="spare")
-        for first in (True, False):
-            nc.tensor.matmul_mx(
-                out=unread[:],
-                lhsT=x_codes[1][:, :P].bitcast(FP8X4),
-                lhsT_scale=x_scales[1][:, :P],
-                rhs=x_codes[0][:].bitcast(FP8X4),
-                rhs_scale=x_scales[0][:],
-                start=first,
-                stop=not first,
-            )
+        def unread_passes(name, tag, count):
+            unread = psum.tile([P, HALF], F32, name=name, tag=tag)
+            for turn in range(count):
+                nc.tensor.matmul_mx(
+                    out=unread[:],
+                    lhsT=stationary[0, 0].bitcast(FP8X4),
+                    lhsT_scale=w_scales[0][:, :P],
+                    rhs=x_codes[0][:, :HALF].bitcast(FP8X4),
+                    rhs_scale=x_scales[0][:, :HALF],
+                    start=(turn == 0),
+                    stop=(turn == count - 1),
+                )
 
         pairs = [slice(0, 2), slice(2, PACK)]
-        for planes in pairs:
-            deal(0, 0, P, DEAL_VECTOR_PASS0, planes)
-        for t0, t1 in ((0, 2), (2, LAST_PLANE)):
-            quantise_w(0, t0, t1, w_codes[0][:, P * t0 : P * t1])
-            for t in range(t0, t1):
-                for piece in range(len(spans[t])):
-                    first_product(0, t, piece)
+        deal(0, 0, P, DEAL_VECTOR_PASS0, slice(0, PACK))
+        quantise_w(0, 0, PACK, w_codes[0][:])
+        unread_passes("unread_first", "spare", 1)
+        for t in range(PACK):
+            for piece in range(len(spans[t])):
+                first_product(0, t, piece)
+
+        quarters = [slice(0, CHUNK), slice(CHUNK, HALF)]
+        for points in quarters:
+            gather(late_rows[0][:, 1, points], 1, 3, points)
+        nc.scalar.activation(late_rows[1][:, 1, :], x_window[1, 3].indirect(offsets[:, HALF // 16 :]), ACT.Copy)
+        for points in quarters:
+            weave(nc.vector.tensor_copy, last_picked[0][:, points, 2:4], late_rows[0][:, :, points])
+        share = LATE_WEAVE_VECTOR
+        weave(nc.vector.tensor_copy, last_picked[1][:, :share, 2:4], late_rows[1][:, :, :share])
+        weave(nc.scalar.copy, last_picked[1][:, share:, 2:4], late_rows[1][:, :, share:])
+        for h, points in enumerate(halves):
+            quantise_x(1, points, last_picked[h][:])
+
         deal(1, 0, M_HALF, DEAL_VECTOR_FIRST_HALF, slice(0, PACK))
         for planes in pairs:
             deal(1, M_HALF, P, DEAL_VECTOR_SECOND_HALF, planes)
         for t in range(PACK):
             quantise_w(1, t, t + 1, w_codes[1][:, P * t : P * (t + 1)])
-        late_codes = sbuf("late_codes", [P, P], U32, tag="w_rows1%d" % M_HALF, align=PACKET)
-        quantise_w(0, LAST_PLANE, PACK, late_codes[:])
         for t in range(PACK):
             for piece in range(len(spans[t])):
-                for g in pass_order[t][t != LAST_PLANE :]:
-                    first_product(g, t, piece)
+                first_product(1, t, piece)
 
         neg_gain = sbuf("neg_gain", [P, PACK], F32, tag="w_codes1")
         nc.gpsimd.tensor_scalar(neg_gain[:], gain[:], -1.0, 0.0, ALU.mult, ALU.add)
@@ -247,6 +251,7 @@ def tile_picked_inorm_none_e_kernel(tc, xT, w1, w2_words, w2_scales, gamma, offs
                 scale=-1.0,
                 accum_out=scalar_moments[key][:, 1:2],
             )
+        unread_passes("unread_second", "bank%d0" % SCALAR_PLANE, 4)
         affine = {}
         inv_std = {}
         for t in (0, 2, SCALAR_PLANE, LAST_PLANE):

@@ -28,9 +28,9 @@ PACKET = 4096
 BN_STATS = 6
 
 DEAL_VECTOR_PASS0 = 84
-DEAL_VECTOR_FIRST_HALF = 20
+DEAL_VECTOR_FIRST_HALF = 14
 DEAL_VECTOR_SECOND_HALF = 42
-LATE_WEAVE_VECTOR = 96
+LATE_WEAVE_VECTOR = 72
 SCALAR_PLANE = 1
 LAST_PLANE = PACK - 1
 
@@ -209,14 +209,18 @@ def tile_picked_inorm_none_e_kernel(tc, xT, w1, w2_words, w2_scales, gamma, offs
         quarters = [slice(0, CHUNK), slice(CHUNK, HALF)]
         for points in quarters:
             gather(late_rows[0][:, 1, points], 1, 3, points)
-        nc.scalar.activation(late_rows[1][:, 1, :], x_window[1, 3].indirect(offsets[:, HALF // 16 :]), ACT.Copy)
+        for points in quarters:
+            entries = offsets[:, (HALF + points.start) // 16 : (HALF + points.stop) // 16]
+            nc.scalar.activation(late_rows[1][:, 1, points], x_window[1, 3].indirect(entries), ACT.Copy)
         for points in quarters:
             weave(nc.vector.tensor_copy, last_picked[0][:, points, 2:4], late_rows[0][:, :, points])
-        share = LATE_WEAVE_VECTOR
-        weave(nc.vector.tensor_copy, last_picked[1][:, :share, 2:4], late_rows[1][:, :, :share])
-        weave(nc.scalar.copy, last_picked[1][:, share:, 2:4], late_rows[1][:, :, share:])
-        for h, points in enumerate(halves):
-            quantise_x(1, points, last_picked[h][:])
+        cut = HALF - LATE_WEAVE_VECTOR
+        for points in (quarters[0], slice(CHUNK, cut)):
+            weave(nc.scalar.copy, last_picked[1][:, points, 2:4], late_rows[1][:, :, points])
+        quantise_x(1, quarters[0], last_picked[0][:, quarters[0]])
+        weave(nc.vector.tensor_copy, last_picked[1][:, cut:, 2:4], late_rows[1][:, :, cut:])
+        quantise_x(1, quarters[1], last_picked[0][:, quarters[1]])
+        quantise_x(1, halves[1], last_picked[1][:])
 
         deal(1, 0, M_HALF, DEAL_VECTOR_FIRST_HALF, slice(0, PACK))
         for planes in pairs:

@@ -185,23 +185,9 @@ def tile_picked_inorm_none_e_kernel(tc, xT, w1, w2_words, w2_scales, gamma, offs
                 stop=(g == pass_order[t][-1]),
             )
 
-        def unread_passes(name, tag, count):
-            unread = psum.tile([P, HALF], F32, name=name, tag=tag)
-            for turn in range(count):
-                nc.tensor.matmul_mx(
-                    out=unread[:],
-                    lhsT=stationary[0, 0].bitcast(FP8X4),
-                    lhsT_scale=w_scales[0][:, :P],
-                    rhs=x_codes[0][:, :HALF].bitcast(FP8X4),
-                    rhs_scale=x_scales[0][:, :HALF],
-                    start=(turn == 0),
-                    stop=(turn == count - 1),
-                )
-
         pairs = [slice(0, 2), slice(2, PACK)]
         deal(0, 0, P, DEAL_VECTOR_PASS0, slice(0, PACK))
         quantise_w(0, 0, PACK, w_codes[0][:])
-        unread_passes("unread_first", "spare", 1)
         for t in range(PACK):
             for piece in range(len(spans[t])):
                 first_product(0, t, piece)
@@ -255,7 +241,6 @@ def tile_picked_inorm_none_e_kernel(tc, xT, w1, w2_words, w2_scales, gamma, offs
                 scale=-1.0,
                 accum_out=scalar_moments[key][:, 1:2],
             )
-        unread_passes("unread_second", "bank%d0" % SCALAR_PLANE, 4)
         affine = {}
         inv_std = {}
         for t in (0, 2, SCALAR_PLANE, LAST_PLANE):

@@ -30,7 +30,7 @@ BN_STATS = 6
 DEAL_VECTOR_PASS0 = 84
 DEAL_VECTOR_FIRST_HALF = 14
 DEAL_VECTOR_SECOND_HALF = 42
-LATE_WEAVE_VECTOR = 72
+LATE_WEAVE_VECTOR = 104
 SCALAR_PLANE = 1
 LAST_PLANE = PACK - 1
 

@@ -281,11 +281,12 @@ def tile_picked_inorm_none_e_kernel(tc, xT, w1, w2_words, w2_scales, gamma, offs
         coefficients(2)
         normalise_vector(0, scaled_copy[0, 0][:], halves[0], copy_factor(0))
         coefficients(SCALAR_PLANE)
-        normalise_vector(2, hidden[2, 0][:], halves[0], psum_factor(2))
+        early, late = slice(0, HALF - CHUNK // 2), slice(HALF - CHUNK // 2, HALF)
+        normalise_vector(2, hidden[2, 0][:, early], early, psum_factor(2))
         coefficients(LAST_PLANE)
-        normalise_vector(SCALAR_PLANE, scaled_copy[SCALAR_PLANE, 0][:, :HALF], halves[0], copy_factor(SCALAR_PLANE))
+        normalise_vector(SCALAR_PLANE, scaled_copy[SCALAR_PLANE, 0][:, :CHUNK], chunks[0], copy_factor(SCALAR_PLANE))
         normalise_vector(LAST_PLANE, hidden[LAST_PLANE, 0][:, chunks[0]], chunks[0], psum_factor(LAST_PLANE))
-        normalise_vector(SCALAR_PLANE, scaled_copy[SCALAR_PLANE, 0][:, HALF:], halves[1], copy_factor(SCALAR_PLANE))
+        normalise_vector(SCALAR_PLANE, scaled_copy[SCALAR_PLANE, 0][:, CHUNK:], slice(CHUNK, S), copy_factor(SCALAR_PLANE))
         for t in (0, 2, LAST_PLANE):
             normalise_scalar(t, hidden[t, 1][:], halves[1])
         normalise_scalar(LAST_PLANE, hidden[LAST_PLANE, 0][:, chunks[1]], chunks[1])
@@ -326,10 +327,11 @@ def tile_picked_inorm_none_e_kernel(tc, xT, w1, w2_words, w2_scales, gamma, offs
         weave_z(nc.vector.tensor_copy, 0, 0, CHUNK)
         weave_z(nc.scalar.copy, 3, 0, CHUNK)
         weave_z(nc.vector.tensor_copy, 2, 0, CHUNK)
-        weave_z(nc.scalar.copy, 1, CHUNK // 2, CHUNK)
+        weave_z(nc.scalar.copy, 1, 0, CHUNK // 2)
         quantise_z(0)
-        weave_z(nc.vector.tensor_copy, 1, 0, CHUNK // 2)
+        normalise_vector(2, hidden[2, 0][:, late], late, psum_factor(2))
         quantise_z(2)
+        weave_z(nc.vector.tensor_copy, 1, CHUNK // 2, CHUNK)
         quantise_z(3)
         quantise_z(1)
         second_product(0, [nc.scalar.copy, nc.scalar.copy], [slice(0, 1), slice(1, 2)])

@@ -85,8 +85,6 @@ def tile_picked_inorm_none_e_kernel(tc, xT, w1, w2_words, w2_scales, gamma, offs
 
         warm_in = sbuf("warm_in", [P, 1], F32)
         warm_out = sbuf("warm_out", [P, 1], F32)
-        nc.vector.memset(warm_in[:], 1.0)
-        nc.scalar.activation(warm_out[:], warm_in[:], ACT.Abs_reciprocal_sqrt, bias=EPS)
 
         constants = {0: (-float(HALF), -1.0), SCALAR_PLANE: (-float(S),), 2: (-1.0,), LAST_PLANE: (-1.0,)}
         moments, mean_at = {}, {}
@@ -94,7 +92,16 @@ def tile_picked_inorm_none_e_kernel(tc, xT, w1, w2_words, w2_scales, gamma, offs
             mean_at[t] = len(constants[t])
             moments[t] = sbuf("moments%d" % t, [P, mean_at[t] + 2], F32)
             for at, value in enumerate(constants[t]):
-                nc.vector.memset(moments[t][:, at : at + 1], value)
+                nc.gpsimd.memset(moments[t][:, at : at + 1], value)
+
+        triples = {
+            0: sbuf("triples0", [P, BN_STATS + 3], F32),
+            2: sbuf("triples2", [P, 2 * BN_STATS], F32),
+            LAST_PLANE: sbuf("triples3", [P, 2 * BN_STATS], F32),
+        }
+        nc.gpsimd.memset(triples[0][:, BN_STATS : BN_STATS + 1], float(HALF))
+        nc.gpsimd.memset(warm_in[:], 1.0)
+        nc.scalar.activation(warm_out[:], warm_in[:], ACT.Abs_reciprocal_sqrt, bias=EPS)
 
         halves = [slice(0, HALF), slice(HALF, S)]
         all_points = slice(0, S)
@@ -122,18 +129,17 @@ def tile_picked_inorm_none_e_kernel(tc, xT, w1, w2_words, w2_scales, gamma, offs
         first_picked = sbuf("first_picked", [P, S, PACK], BF16)
         for j in range(PACK):
             gather(first_rows[:, j, :], 0, j, all_points)
-        weave(nc.vector.tensor_copy, first_picked[:, :HALF], first_rows[:, :, :HALF])
-        weave(nc.scalar.copy, first_picked[:, HALF:], first_rows[:, :, HALF:])
+        weave(nc.vector.tensor_copy, first_picked[:], first_rows[:])
         early_rows = sbuf("early_rows", [P, 2, S], F32)
         for j in range(2):
             gather(early_rows[:, j, :], 1, j, all_points)
         quantise_x(0, all_points, first_picked[:])
         last_picked = [sbuf("last_picked%d" % h, [P, HALF, PACK], BF16) for h in range(2)]
-        late_rows = [sbuf("late_rows%d" % h, [P, 2, HALF], F32) for h in range(2)]
+        late_all = sbuf("late_rows", [P, 2, S], F32)
+        late_rows = [late_all[:, :, points] for points in halves]
         for h, points in enumerate(halves):
             weave(nc.scalar.copy, last_picked[h][:, :, 0:2], early_rows[:, :, points])
-        for h, points in enumerate(halves):
-            gather(late_rows[h][:, 0, :], 1, 2, points)
+        gather(late_all[:, 0, :], 1, 2, all_points)
 
         spans = {t: [all_points] if t == SCALAR_PLANE else halves for t in range(PACK)}
         hidden = {}
@@ -142,13 +148,6 @@ def tile_picked_inorm_none_e_kernel(tc, xT, w1, w2_words, w2_scales, gamma, offs
                 hidden[t, piece] = psum.tile(
                     [P, points.stop - points.start], F32, name="hidden%d%d" % (t, piece), tag="bank%d%d" % (t, piece)
                 )
-
-        triples = {
-            0: sbuf("triples0", [P, BN_STATS + 3], F32),
-            2: sbuf("triples2", [P, 2 * BN_STATS], F32),
-            LAST_PLANE: sbuf("triples3", [P, 2 * BN_STATS], F32),
-        }
-        nc.vector.memset(triples[0][:, BN_STATS : BN_STATS + 1], float(HALF))
 
         w_codes = [sbuf("w_codes0", [P, H], U32), sbuf("w_codes1", [P, H], U32)]
         w_scales = [sbuf("w_scales%d" % g, [P, H], U8) for g in range(PASSES)]
@@ -217,8 +216,8 @@ def tile_picked_inorm_none_e_kernel(tc, xT, w1, w2_words, w2_scales, gamma, offs
             for piece in range(len(spans[t])):
                 first_product(1, t, piece)
 
-        neg_gain = sbuf("neg_gain", [P, PACK], F32, tag="w_codes1")
-        nc.gpsimd.tensor_scalar(neg_gain[:], gain[:], -1.0, 0.0, ALU.mult, ALU.add)
+        neg_gain = sbuf("neg_gain", [P, PACK], F32)
+        nc.scalar.activation(neg_gain[:], gain[:], ACT.Identity, scale=-1.0)
         z_planes = sbuf("z_planes", [P, PACK, S], BF16)
 
         scaled_copy = {(0, 0): sbuf("scaled_copy0", [P, HALF], F32), (SCALAR_PLANE, 0): sbuf("scaled_copy1", [P, S], F32)}

@@ -38,7 +38,9 @@ LAST_PLANE = PACK - 1
 def tile_picked_inorm_none_e_kernel(tc, xT, w1, w2_words, w2_scales, gamma, offs, out):
     nc = tc.nc
     with ExitStack() as ctx:
+        low = ctx.enter_context(tc.tile_pool(name="low", bufs=1))
         keep = ctx.enter_context(tc.tile_pool(name="keep", bufs=1))
+        high = ctx.enter_context(tc.tile_pool(name="high", bufs=1))
         psum = ctx.enter_context(tc.psum_pool(name="psum", bufs=1))
 
         def sbuf(name, shape, dtype, tag=None, align=256):
@@ -52,14 +54,20 @@ def tile_picked_inorm_none_e_kernel(tc, xT, w1, w2_words, w2_scales, gamma, offs
         x_window = {}
         w_raw = {}
 
+        landed = []
+
+        def landing(name, shape):
+            landed.append(name)
+            return (high, low)[len(landed) % 2].tile(shape, F32, name=name, align_bytes=PACKET)
+
         def load_x(g, j0, rows):
-            loaded = sbuf("x_rows%d%d" % (g, j0), [P, rows, T], F32, align=PACKET)
+            loaded = landing("x_rows%d%d" % (g, j0), [P, rows, T])
             nc.sync.dma_start(out=loaded[:], in_=x_rows[g][:, j0 : j0 + rows])
             for j in range(rows):
                 x_window[g, j0 + j] = loaded[:, j, :]
 
         def load_w(g, m0, m1):
-            w_raw[g, m0] = sbuf("w_rows%d%d" % (g, m0), [P, PACK, PACK * (m1 - m0)], F32, align=PACKET)
+            w_raw[g, m0] = landing("w_rows%d%d" % (g, m0), [P, PACK, PACK * (m1 - m0)])
             nc.sync.dma_start(out=w_raw[g, m0][:], in_=w_rows[g][:, :, PACK * m0 : PACK * m1])
 
         load_x(0, 0, 2)

from contextlib import ExitStack

import concourse.mybir as mybir

K, T, S, H, N = 1024, 2048, 512, 512, 256
FLOPS = 2 * K * H * S + 2 * H * N * S
EPS = 1e-5

F32 = mybir.dt.float32
BF16 = mybir.dt.bfloat16
I32 = mybir.dt.int32
U32 = mybir.dt.uint32
U16 = mybir.dt.uint16
U8 = mybir.dt.uint8
FP8X4 = mybir.dt.float8_e4m3fn_x4
FP4X4 = mybir.dt.float4_e2m1fn_x4
ACT = mybir.ActivationFunctionType
ALU = mybir.AluOpType

P = 128
PACK = 4
PASSES = K // (P * PACK)
HALF = S // 2
CHUNK = 128
CHUNKS = S // CHUNK
M_HALF = P // 2
PACKET = 4096
BN_STATS = 6

DEAL_VECTOR_PASS0 = 84
DEAL_VECTOR_FIRST_HALF = 14
DEAL_VECTOR_SECOND_HALF = 42
LATE_WEAVE_VECTOR = 104
SCALAR_PLANE = 1
LAST_PLANE = PACK - 1


def tile_picked_inorm_none_e_kernel(tc, xT, w1, w2_words, w2_scales, gamma, offs, out):
    nc = tc.nc
    with ExitStack() as ctx:
        low = ctx.enter_context(tc.tile_pool(name="low", bufs=1))
        keep = ctx.enter_context(tc.tile_pool(name="keep", bufs=1))
        high = ctx.enter_context(tc.tile_pool(name="high", bufs=1))
        psum = ctx.enter_context(tc.psum_pool(name="psum", bufs=1))

        def sbuf(name, shape, dtype, tag=None, align=256):
            return keep.tile(shape, dtype, name=name, tag=tag or name, align_bytes=align)

        offsets = keep.tile([P, S // 16], U16, name="offsets")
        gain = sbuf("gain", [P, PACK], F32)
        x_rows = xT.rearrange("(g p j) t -> g p j t", p=P, j=PACK)
        w_rows = w1.rearrange("(g p j) c -> g p j c", p=P, j=PACK)

        x_window = {}
        w_raw = {}

        landed = []

        def landing(name, shape):
            landed.append(name)
            return (high, low)[len(landed) % 2].tile(shape, F32, name=name, align_bytes=PACKET)

        def load_x(g, j0, rows):
            loaded = landing("x_rows%d%d" % (g, j0), [P, rows, T])
            nc.sync.dma_start(out=loaded[:], in_=x_rows[g][:, j0 : j0 + rows])
            for j in range(rows):
                x_window[g, j0 + j] = loaded[:, j, :]

        def load_w(g, m0, m1):
            w_raw[g, m0] = landing("w_rows%d%d" % (g, m0), [P, PACK, PACK * (m1 - m0)])
            nc.sync.dma_start(out=w_raw[g, m0][:], in_=w_rows[g][:, :, PACK * m0 : PACK * m1])

        load_x(0, 0, 2)
        nc.sync.dma_start(offsets[:], offs)
        load_x(0, 2, 2)
        load_x(1, 0, 2)
        load_x(1, 2, 1)
        load_w(0, 0, P)
        load_x(1, 3, 1)
        load_w(1, 0, M_HALF)
        load_w(1, M_HALF, P)
        nc.sync.dma_start(out=gain[:], in_=gamma.rearrange("(p t) o -> p (t o)", t=PACK))
        w2_codes = sbuf("w2_codes", [P, 2 * N], U8)
        nc.sync.dma_start(out=w2_codes[:].bitcast(I32), in_=w2_words[0].bitcast(I32))
        w2_scale_rows = sbuf("w2_scale_rows", [P, N], U8)
        nc.gpsimd.memset(w2_scale_rows[:], 0)
        for row in range(0, 16, 2):
            place = 32 * (row // 4) + row % 4
            nc.sync.dma_start(
                out=w2_scale_rows[place : place + 2, :].bitcast(I32),
                in_=w2_scales[0, row : row + 2, :].bitcast(I32),
            )

        warm_in = sbuf("warm_in", [P, 1], F32)
        warm_out = sbuf("warm_out", [P, 1], F32)

        constants = {0: (-float(HALF), -1.0), SCALAR_PLANE: (-float(S),), 2: (-1.0,), LAST_PLANE: (-1.0,)}
        moments, mean_at = {}, {}
        for t in range(PACK):
            mean_at[t] = len(constants[t])
            moments[t] = sbuf("moments%d" % t, [P, mean_at[t] + 2], F32)
            for at, value in enumerate(constants[t]):
                nc.gpsimd.memset(moments[t][:, at : at + 1], value)

        triples = {
            0: sbuf("triples0", [P, BN_STATS + 3], F32),
            2: sbuf("triples2", [P, 2 * BN_STATS], F32),
            LAST_PLANE: sbuf("triples3", [P, 2 * BN_STATS], F32),
        }
        nc.gpsimd.memset(triples[0][:, BN_STATS : BN_STATS + 1], float(HALF))
        nc.gpsimd.memset(warm_in[:], 1.0)
        nc.scalar.activation(warm_out[:], warm_in[:], ACT.Abs_reciprocal_sqrt, bias=EPS)

        halves = [slice(0, HALF), slice(HALF, S)]
        all_points = slice(0, S)
        x_codes = [sbuf("x_codes%d" % g, [P, S], U32) for g in range(PASSES)]
        x_scales = [sbuf("x_scales%d" % g, [P, S], U8) for g in range(PASSES)]

        def gather(target, g, j, points):
            entries = offsets[:, points.start // 16 : points.stop // 16]
            nc.vector.tensor_copy(target, x_window[g, j].indirect(entries))

        def weave(copy, target, source, run=4):
            copy(
                out=target.rearrange("p (c i) j -> p c j i", i=run),
                in_=source.rearrange("p j (c i) -> p c j i", i=run),
            )

        def quantise_x(g, points, source):
            nc.vector.quantize_mx(
                out=x_codes[g][:, points].bitcast(FP8X4),
                scales=x_scales[g][:, points],
                in_=source.rearrange("p s j -> p (s j)"),
            )

        first_rows = sbuf("first_rows", [P, PACK, S], F32)
        first_picked = sbuf("first_picked", [P, S, PACK], BF16)
        for j in range(PACK):
            gather(first_rows[:, j, :], 0, j, all_points)
        weave(nc.vector.tensor_copy, first_picked[:], first_rows[:])
        early_rows = sbuf("early_rows", [P, 2, S], F32)
        for j in range(2):
            gather(early_rows[:, j, :], 1, j, all_points)
        quantise_x(0, all_points, first_picked[:])
        last_picked = [sbuf("last_picked%d" % h, [P, HALF, PACK], BF16) for h in range(2)]
        late_all = sbuf("late_rows", [P, 2, S], F32)
        late_rows = [late_all[:, :, points] for points in halves]
        for h, points in enumerate(halves):
            weave(nc.scalar.copy, last_picked[h][:, :, 0:2], early_rows[:, :, points])
        gather(late_all[:, 0, :], 1, 2, all_points)

        spans = {t: [all_points] if t == SCALAR_PLANE else halves for t in range(PACK)}
        hidden = {}
        for t in range(PACK):
            for piece, points in enumerate(spans[t]):
                hidden[t, piece] = psum.tile(
                    [P, points.stop - points.start], F32, name="hidden%d%d" % (t, piece), tag="bank%d%d" % (t, piece)
                )

        w_codes = [sbuf("w_codes0", [P, H], U32), sbuf("w_codes1", [P, H], U32)]
        w_scales = [sbuf("w_scales%d" % g, [P, H], U8) for g in range(PASSES)]
        dealt = [sbuf("dealt%d" % g, [P, PACK, P, PACK], BF16) for g in range(PASSES)]

        def deal(g, m0, m1, vector_share, planes):
            source = w_raw[g, m0][:].rearrange("p j (m t) -> p m j t", t=PACK)[:, :, :, planes]
            target = dealt[g][:, planes, m0:m1, :].rearrange("p t m j -> p m j t")
            nc.vector.tensor_copy(out=target[:, :vector_share], in_=source[:, :vector_share])
            nc.scalar.copy(out=target[:, vector_share:], in_=source[:, vector_share:])

        stationary = {}

        def quantise_w(g, t0, t1, codes):
            nc.vector.quantize_mx(
                out=codes.bitcast(FP8X4),
                scales=w_scales[g][:, P * t0 : P * t1],
                in_=dealt[g][:, t0:t1].rearrange("p t m j -> p (t m j)"),
            )
            for t in range(t0, t1):
                stationary[g, t] = codes[:, P * (t - t0) : P * (t - t0 + 1)]

        pass_order = {t: (0, 1) for t in range(PACK)}

        def first_product(g, t, piece):
            points = spans[t][piece]
            nc.tensor.matmul_mx(
                out=hidden[t, piece][:],
                lhsT=stationary[g, t].bitcast(FP8X4),
                lhsT_scale=w_scales[g][:, P * t : P * (t + 1)],
                rhs=x_codes[g][:, points].bitcast(FP8X4),
                rhs_scale=x_scales[g][:, points],
                start=(g == pass_order[t][0]),
                stop=(g == pass_order[t][-1]),
            )

        pairs = [slice(0, 2), slice(2, PACK)]
        deal(0, 0, P, DEAL_VECTOR_PASS0, slice(0, PACK))
        quantise_w(0, 0, PACK, w_codes[0][:])
        for t in range(PACK):
            for piece in range(len(spans[t])):
                first_product(0, t, piece)

        quarters = [slice(0, CHUNK), slice(CHUNK, HALF)]
        for points in quarters:
            gather(late_rows[0][:, 1, points], 1, 3, points)
        for points in quarters:
            entries = offsets[:, (HALF + points.start) // 16 : (HALF + points.stop) // 16]
            nc.scalar.activation(late_rows[1][:, 1, points], x_window[1, 3].indirect(entries), ACT.Copy)
        for points in quarters:
            weave(nc.vector.tensor_copy, last_picked[0][:, points, 2:4], late_rows[0][:, :, points])
        cut = HALF - LATE_WEAVE_VECTOR
        for points in (quarters[0], slice(CHUNK, cut)):
            weave(nc.scalar.copy, last_picked[1][:, points, 2:4], late_rows[1][:, :, points])
        quantise_x(1, quarters[0], last_picked[0][:, quarters[0]])
        weave(nc.vector.tensor_copy, last_picked[1][:, cut:, 2:4], late_rows[1][:, :, cut:])
        quantise_x(1, quarters[1], last_picked[0][:, quarters[1]])
        quantise_x(1, halves[1], last_picked[1][:])

        deal(1, 0, M_HALF, DEAL_VECTOR_FIRST_HALF, slice(0, PACK))
        for planes in pairs:
            deal(1, M_HALF, P, DEAL_VECTOR_SECOND_HALF, planes)
        for t in range(PACK):
            quantise_w(1, t, t + 1, w_codes[1][:, P * t : P * (t + 1)])
        for t in range(PACK):
            for piece in range(len(spans[t])):
                first_product(1, t, piece)

        neg_gain = sbuf("neg_gain", [P, PACK], F32)
        nc.scalar.activation(neg_gain[:], gain[:], ACT.Identity, scale=-1.0)
        z_planes = sbuf("z_planes", [P, PACK, S], BF16)

        scaled_copy = {(0, 0): sbuf("scaled_copy0", [P, HALF], F32), (SCALAR_PLANE, 0): sbuf("scaled_copy1", [P, S], F32)}
        squares = sbuf("squares", [P, HALF + S], F32)
        scalar_moments = {
            (0, 0): triples[0][:, BN_STATS + 1 :],
            (SCALAR_PLANE, 0): moments[SCALAR_PLANE][:, mean_at[SCALAR_PLANE] :],
        }
        squares_part = {(0, 0): squares[:, :HALF], (SCALAR_PLANE, 0): squares[:, HALF:]}
        for key, target in scaled_copy.items():
            nc.scalar.activation(
                target[:], hidden[key][:], ACT.Identity, scale=1.0 / target.shape[1], accum_out=scalar_moments[key][:, 0:1]
            )
        for key in scaled_copy:
            nc.scalar.activation(
                squares_part[key],
                hidden[key][:],
                ACT.Square,
                bias=scalar_moments[key][:, 0:1],
                scale=-1.0,
                accum_out=scalar_moments[key][:, 1:2],
            )
        affine = {}
        inv_std = {}
        for t in (0, 2, SCALAR_PLANE, LAST_PLANE):
            inv_std[t] = sbuf("inv_std%d" % t, [P, 1], F32)
            spread = moments[t][:, mean_at[t] + 1 :]
            if t == SCALAR_PLANE:
                nc.scalar.activation(inv_std[t][:], spread, ACT.Abs_reciprocal_sqrt, bias=EPS, scale=1.0 / S)
            else:
                by_vector = [half for half in range(2) if (t, half) not in scaled_copy]
                for n, half in enumerate(by_vector):
                    nc.vector.bn_stats(triples[t][:, BN_STATS * n : BN_STATS * (n + 1)], hidden[t, half][:])
                nc.vector.bn_aggr(moments[t][:, mean_at[t] :], triples[t][:])
                nc.scalar.activation(inv_std[t][:], spread, ACT.Abs_reciprocal_sqrt, bias=EPS)

        def coefficients(t):
            affine[t] = sbuf("affine%d" % t, [P, mean_at[t] + 1], F32)
            nc.vector.tensor_scalar(
                affine[t][:], moments[t][:, : mean_at[t] + 1], inv_std[t][:], neg_gain[:, t : t + 1], ALU.mult, ALU.mult
            )

        def shift(t):
            return affine[t][:, mean_at[t] :]

        def copy_factor(t):
            return affine[t][:, 0:1]

        def psum_factor(t):
            return affine[t][:, mean_at[t] - 1 : mean_at[t]]

        def normalise_vector(t, source, points, factor):
            nc.vector.tensor_scalar(z_planes[:, t, points], source, factor, shift(t), ALU.mult, ALU.add)

        def normalise_scalar(t, source, points):
            nc.scalar.activation(z_planes[:, t, points], source, ACT.Identity, bias=shift(t), scale=psum_factor(t))

        chunks = [slice(c * CHUNK, (c + 1) * CHUNK) for c in range(CHUNKS)]
        coefficients(0)
        coefficients(2)
        normalise_vector(0, scaled_copy[0, 0][:], halves[0], copy_factor(0))
        coefficients(SCALAR_PLANE)
        early, late = slice(0, HALF - CHUNK // 2), slice(HALF - CHUNK // 2, HALF)
        normalise_vector(2, hidden[2, 0][:, early], early, psum_factor(2))
        coefficients(LAST_PLANE)
        normalise_vector(SCALAR_PLANE, scaled_copy[SCALAR_PLANE, 0][:, :CHUNK], chunks[0], copy_factor(SCALAR_PLANE))
        normalise_vector(LAST_PLANE, hidden[LAST_PLANE, 0][:, chunks[0]], chunks[0], psum_factor(LAST_PLANE))
        normalise_vector(SCALAR_PLANE, scaled_copy[SCALAR_PLANE, 0][:, CHUNK:], slice(CHUNK, S), copy_factor(SCALAR_PLANE))
        for t in (0, 2, LAST_PLANE):
            normalise_scalar(t, hidden[t, 1][:], halves[1])
        normalise_scalar(LAST_PLANE, hidden[LAST_PLANE, 0][:, chunks[1]], chunks[1])

        woven = [sbuf("woven%d" % c, [P, CHUNK, PACK], BF16) for c in range(CHUNKS)]
        z_codes = [sbuf("z_codes%d" % c, [P, CHUNK], U32) for c in range(CHUNKS)]
        z_scales = [sbuf("z_scales%d" % c, [P, CHUNK], U8) for c in range(CHUNKS)]
        out_rows = out.rearrange("(m p) s -> p m s", p=P)
        banks = ["spare"] + ["bank%d%d" % key for key in hidden]

        def weave_z(copy, c, s0, s1):
            weave(copy, woven[c][:, s0:s1, :], z_planes[:, :, c * CHUNK + s0 : c * CHUNK + s1], run=8)

        def quantise_z(c):
            nc.vector.quantize_mx(
                out=z_codes[c][:].bitcast(FP8X4),
                scales=z_scales[c][:],
                in_=woven[c][:].rearrange("p s t -> p (s t)"),
            )

        def second_product(c, copies, stores):
            result = sbuf("result%d" % c, [P, N // P, CHUNK], F32)
            for m, copy in enumerate(copies):
                acc = psum.tile([P, CHUNK], F32, name="acc%d%d" % (c, m), tag=banks[2 * c + m])
                nc.tensor.matmul_mx(
                    out=acc[:],
                    lhsT=w2_codes[:, 2 * P * m : 2 * P * (m + 1)].bitcast(FP4X4),
                    lhsT_scale=w2_scale_rows[:, P * m : P * (m + 1)],
                    rhs=z_codes[c][:].bitcast(FP8X4),
                    rhs_scale=z_scales[c][:],
                    start=True,
                    stop=True,
                )
                copy(out=result[:, m, :], in_=acc[:])
            for blocks in stores:
                nc.sync.dma_start(out=out_rows[:, blocks, c * CHUNK : (c + 1) * CHUNK], in_=result[:, blocks, :])

        weave_z(nc.vector.tensor_copy, 0, 0, CHUNK)
        weave_z(nc.scalar.copy, 3, 0, CHUNK)
        weave_z(nc.vector.tensor_copy, 2, 0, CHUNK)
        weave_z(nc.scalar.copy, 1, 0, CHUNK // 2)
        quantise_z(0)
        normalise_vector(2, hidden[2, 0][:, late], late, psum_factor(2))
        quantise_z(2)
        weave_z(nc.vector.tensor_copy, 1, CHUNK // 2, CHUNK)
        quantise_z(3)
        quantise_z(1)
        second_product(0, [nc.scalar.copy, nc.scalar.copy], [slice(0, 1), slice(1, 2)])
        for c in (2, 3, 1):
            second_product(c, [nc.scalar.copy, nc.vector.tensor_copy], [slice(0, 2)])
